import numpy as np
import ml_dtypes


def mxq(x, axis, fmt="e4m3"):
    dtype, down = {"e4m3": (ml_dtypes.float8_e4m3fn, 7), "e5m2": (ml_dtypes.float8_e5m2, 14)}[fmt]
    v = np.moveaxis(np.asarray(x, np.float32).astype(ml_dtypes.bfloat16).astype(np.float64), axis, -1)
    blocks = v.reshape(v.shape[:-1] + (-1, 32))
    amax = np.abs(blocks).max(-1, keepdims=True)
    byte = np.maximum(np.where(amax > 0, np.frexp(amax)[1] - 1 + 127, 0) - down, 1)
    scale = np.exp2(byte - 127.0)
    codes = (blocks / scale).astype(np.float32).astype(dtype).astype(np.float64)
    return np.moveaxis((codes * scale).reshape(v.shape), -1, axis)


WIDE = False


def mx_kscale(k):
    if not WIDE:
        return np.ones(k)
    levels = np.array([10, -10, 5, -5, 0])
    if k % 512:
        return np.exp2(np.random.permutation(np.resize(levels, k // 32))).repeat(32)
    a = np.empty((k // 512, 16))
    for p in range(k // 512):
        a[p, :8] = np.random.permutation(np.resize(levels, 8))
        for g in range(8):
            far = levels[np.abs(levels - a[p, g]) >= 10]
            a[p, g + 8] = far[np.random.randint(len(far))]
    return np.exp2(a.ravel()).repeat(32)


def f64(x):
    return np.asarray(x).astype(np.float64)


def striped(idx):
    return np.tile(np.asarray(idx).reshape(-1, 16).T, (8, 1)).astype(np.uint16)


def unstriped(offs):
    return offs[:16].T.reshape(-1).astype(np.int64)


E2M1 = np.array([0.0, 0.5, 1.0, 1.5, 2.0, 3.0, 4.0, 6.0, -0.0, -0.5, -1.0, -1.5, -2.0, -3.0, -4.0, -6.0])


def pack_weight(w, fmt):
    k, n = w.shape
    w = f64(np.asarray(w, np.float32).astype(ml_dtypes.bfloat16)).reshape(k // 32, 32, n)
    amax = np.abs(w).max(1)
    if fmt == "e4m3":
        byte = np.frexp(amax)[1] - 1 + 127 - 7
    else:
        mant, ex = np.frexp(amax / 6.0)
        byte = np.where(mant > 0.5, ex, ex - 1) + 127
    byte = np.clip(np.where(amax > 0, byte, 1), 1, 254)
    scaled = (w * np.exp2(127.0 - byte)[:, None, :]).reshape(k, n).astype(np.float32)
    by_word = np.ascontiguousarray(scaled.reshape(k // 512, 128, 4, n).transpose(0, 1, 3, 2))
    if fmt == "e4m3":
        words = by_word.astype(ml_dtypes.float8_e4m3fn).view(np.uint8)
    else:
        c = by_word.astype(ml_dtypes.float4_e2m1fn).view(np.uint8) & 0xF
        words = (c[..., 0::2] | (c[..., 1::2] << 4)).reshape(k // 512, 128, 2 * n)
    return np.ascontiguousarray(words), np.ascontiguousarray(byte.astype(np.uint8).reshape(k // 512, 16, n))


def unpack_weight(words, scales, fmt):
    g, _, n = scales.shape
    words = np.ascontiguousarray(words).reshape(g, 128, n, -1)
    if fmt == "e4m3":
        vals = words.view(ml_dtypes.float8_e4m3fn).astype(np.float64)
    else:
        nib = np.empty((g, 128, n, 4), np.uint8)
        nib[..., 0::2] = words & 0xF
        nib[..., 1::2] = words >> 4
        vals = E2M1[nib]
    vals = vals * np.repeat(np.exp2(scales.astype(np.float64) - 127.0), 8, axis=1)[..., None]
    return vals.transpose(0, 1, 3, 2).reshape(g * 512, n)


def sigmoid(v):
    return 1.0 / (1.0 + np.exp(-v))


K, R, F, T, J, G = 512, 512, 512, 1024, 256, 64


def setup_inputs():
    n = np.random.standard_normal
    idx = np.random.permutation(T)[:J]
    fk = mx_kscale(K)
    ff = mx_kscale(F)
    fr = mx_kscale(R)
    tabp = pack_weight(n((K, T)) / fk[:, None], "e2m1")
    return {
        "tab_words": tabp[0],
        "tab_scales": tabp[1],
        "w1": (n((K, R)) * 1 / np.sqrt(K) * fk[:, None]).astype(np.float32),
        "temper": (np.random.uniform(0.5, 2.0, (R, 1))).astype(np.float32),
        "wo": (n((F, R)) * 1 / np.sqrt(F) * ff[:, None]).astype(np.float32),
        "dy": (n((F, G)) / ff[:, None]).astype(np.float32),
        "rs": (np.random.uniform(0.5, 2.0, (R, 1)) * fr[:, None]).astype(np.float32),
        "w1r": (n((R, K)) * 1 / np.sqrt(R) / fr[:, None]).astype(np.float32),
        "old": (n((K, T)) * 2.0).astype(np.float32),
        "fade": (np.random.uniform(0.5, 1.0, (1, T))).astype(np.float32),
        "offs": striped(idx),
    }


def reference(tab_words, tab_scales, w1, temper, wo, dy, rs, w1r, old, fade, offs):
    idx = unstriped(offs)
    tabu = unpack_weight(tab_words, tab_scales, "e2m1")
    w1q = mxq(f64(w1), 0, "e4m3")
    tabidxg = tabu[:, idx]
    a = w1q.T @ tabidxg
    p = np.exp(a * f64(temper))
    z = p.reshape(R, G, J // G).sum(axis=2)
    s = np.log(z) / f64(temper)
    woq = mxq(f64(wo), 0, "e4m3")
    dyq = mxq(f64(dy), 0, "e4m3")
    c0 = woq.T @ dyq
    ds = c0 * sigmoid(s) * (1.0 + s * (1.0 - sigmoid(s)))
    dz = ds / f64(temper) / z
    r1 = np.repeat(dz, J // G, axis=1)
    da = r1 * p * f64(temper)
    gs = da * f64(rs)
    w1rq = mxq(f64(w1r), 0, "e4m3")
    gsq = mxq(gs, 0, "e4m3")
    gx1 = w1rq.T @ gsq
    gf = np.zeros((K, T))
    gf[:, idx] = gx1
    y = f64(old) * f64(fade) + gf
    return y

@@ -1,0 +1,268 @@
+from contextlib import ExitStack
+
+import concourse.mybir as mybir
+from concourse.masks import make_identity
+
+K, R, F, T, J, G = 512, 512, 512, 1024, 256, 64
+FLOPS = 2 * (K * R * J + F * R * G + R * K * J)
+
+F32 = mybir.dt.float32
+BF16 = mybir.dt.bfloat16
+I32 = mybir.dt.int32
+U32 = mybir.dt.uint32
+U16 = mybir.dt.uint16
+U8 = mybir.dt.uint8
+FP8X4 = mybir.dt.float8_e4m3fn_x4
+FP4X4 = mybir.dt.float4_e2m1fn_x4
+ACT = mybir.ActivationFunctionType
+ALU = mybir.AluOpType
+AX = mybir.AxisListType
+
+P = 128
+PACK = 4
+POOL = J // G
+HALF_M = P // 2
+W1_VECTOR_M = 40
+
+
+def dealt_views(grouped, raw, m0, m1):
+    out = grouped[:, :, m0:m1, :].rearrange("p t m j -> p m j t")
+    in_ = raw[:].rearrange("p j (m t) -> p m j t", t=PACK)[:, m0:m1, :, :]
+    return out, in_
+
+
+def plain_views(grouped, raw, c0, c1):
+    out = grouped[:].rearrange("p (c i) j -> p c j i", i=PACK)[:, c0:c1, :, :]
+    in_ = raw[:].rearrange("p j (c i) -> p c j i", i=PACK)[:, c0:c1, :, :]
+    return out, in_
+
+
+def tile_attend_csoftmaxpool_x_kernel(tc, tab_words, tab_scales, w1, temper, wo, dy, rs, w1r, old, fade, offs, out):
+    nc = tc.nc
+    with ExitStack() as ctx:
+        keep = ctx.enter_context(tc.tile_pool(name="keep", bufs=1))
+        psum = ctx.enter_context(tc.psum_pool(name="psum", bufs=1))
+
+        def sb(name, shape, dtype):
+            return keep.tile(shape, dtype, name=name, align_bytes=64)
+
+        offsets = keep.tile([P, J // 16], U16, name="offsets")
+        nc.sync.dma_start(offsets[:], offs)
+
+        tab_s = sb("tab_s", [P, T], U8)
+        nc.vector.memset(tab_s[:].bitcast(I32), 0)
+        scale_rows = sb("scale_rows", [P, T // 4], I32)
+        for q in range(4):
+            nc.scalar.dma_start(scale_rows[32 * q : 32 * q + 4, :], tab_scales[0, 4 * q : 4 * q + 4, :].bitcast(I32))
+        tab_w = sb("tab_w", [P, T], U16)
+        nc.sync.dma_start(tab_w[:].bitcast(I32), tab_words[0].bitcast(I32))
+        w1_raw = []
+        for h in range(2):
+            raw = sb(f"w1_raw{h}", [P, PACK, R // 2], F32)
+            nc.sync.dma_start(raw[:], w1[:, h * (R // 2) : (h + 1) * (R // 2)].rearrange("(p j) c -> p j c", j=PACK))
+            w1_raw.append(raw)
+        wo_raw = sb("wo_raw", [P, PACK, R], F32)
+        nc.sync.dma_start(wo_raw[:], wo.rearrange("(p j) c -> p j c", j=PACK))
+        temp = sb("temp", [P, PACK], F32)
+        nc.sync.dma_start(temp[:], temper.rearrange("(p t) o -> p (t o)", t=PACK))
+        dy_raw = sb("dy_raw", [P, PACK, G], F32)
+        nc.sync.dma_start(dy_raw[:], dy.rearrange("(p j) c -> p j c", j=PACK))
+        w1r_raw = sb("w1r_raw", [P, PACK, K], F32)
+        nc.sync.dma_start(w1r_raw[:], w1r.rearrange("(p j) c -> p j c", j=PACK))
+        rs_sb = sb("rs_sb", [P, PACK], F32)
+        nc.sync.dma_start(rs_sb[:], rs.rearrange("(p t) o -> p (t o)", t=PACK))
+        fade_rows = sb("fade_rows", [P, P], F32)
+        nc.gpsimd.memset(fade_rows[:], 0.0)
+        nc.sync.dma_start(fade_rows[0 : T // P, :], fade.rearrange("o (c p) -> (o c) p", p=P))
+        old_sb = []
+        for h in range(2):
+            tile = sb(f"old{h}", [P, 4, T // 2], F32)
+            nc.sync.dma_start(tile[:], old[:, h * (T // 2) : (h + 1) * (T // 2)].rearrange("(a p) c -> p a c", p=P))
+            old_sb.append(tile)
+
+        ident = sb("ident", [P, P], F32)
+        make_identity(nc, ident[:])
+
+        windows = [keep.tile([P, T], F32, name=f"window{a}") for a in range(4)]
+        for a in range(4):
+            (nc.vector if a < 2 else nc.gpsimd).memset(windows[a][:], 0.0)
+        for q in range(4):
+            nc.vector.tensor_copy(tab_s[32 * q : 32 * q + 4, :].bitcast(I32), scale_rows[32 * q : 32 * q + 4, :])
+
+        got_w = sb("got_w", [P, J], U16)
+        nc.vector.tensor_copy(got_w[:], tab_w[:].indirect(offsets[:]))
+        got_s = sb("got_s", [P, J], U8)
+        nc.vector.tensor_copy(got_s[:], tab_s[:].indirect(offsets[:]))
+
+        w1_codes = [sb(f"w1_codes{t}", [P, P], U32) for t in range(PACK)]
+        w1_scales = [sb(f"w1_scales{t}", [P, P], U8) for t in range(PACK)]
+        for h in range(2):
+            grouped = sb(f"w1_grouped{h}", [P, PACK, HALF_M, PACK], BF16)
+            o, i = dealt_views(grouped, w1_raw[h], 0, W1_VECTOR_M)
+            nc.vector.tensor_copy(o, i)
+            o, i = dealt_views(grouped, w1_raw[h], W1_VECTOR_M, HALF_M)
+            nc.scalar.copy(o, i)
+            cols = slice(h * HALF_M, (h + 1) * HALF_M)
+            for t in range(PACK):
+                nc.vector.quantize_mx(
+                    out=w1_codes[t][:, cols].bitcast(FP8X4),
+                    scales=w1_scales[t][:, cols],
+                    in_=grouped[:, t, :, :].rearrange("p m j -> p (m j)"),
+                )
+
+        a_banks = [psum.tile([P, 2, J], F32, name=f"a_bank{b}", tag=f"mx{b}") for b in range(2)]
+        x = [sb(f"x{t}", [P, G, POOL], F32) for t in range(PACK)]
+        for t in range(PACK):
+            nc.tensor.matmul_mx(
+                out=a_banks[t // 2][:, t % 2, :],
+                lhsT=w1_codes[t][:].bitcast(FP8X4),
+                lhsT_scale=w1_scales[t][:],
+                rhs=got_w[:].bitcast(FP4X4),
+                rhs_scale=got_s[:],
+                start=True,
+                stop=True,
+            )
+        for t in range(PACK):
+            nc.scalar.activation(x[t][:].rearrange("p g q -> p (g q)"), a_banks[t // 2][:, t % 2, :], ACT.Copy, scale=temp[:, t : t + 1])
+
+        top = sb("top", [P, PACK, G], F32)
+        below = [sb(f"below{t}", [P, G, POOL], F32) for t in range(PACK)]
+        p_sb = sb("p_sb", [P, PACK, G, POOL], F32)
+        z = sb("z", [P, PACK, G], F32)
+
+        def group_max(t):
+            nc.vector.tensor_reduce(top[:, t, :], x[t][:], AX.X, ALU.max)
+
+        def shifted_exp(t):
+            nc.vector.tensor_tensor(below[t][:], x[t][:], top[:, t, :].unsqueeze(2).to_broadcast([P, G, POOL]), ALU.subtract)
+            nc.scalar.activation(p_sb[:, t, :, :], below[t][:], ACT.Exp)
+
+        group_max(0)
+        for t in range(PACK):
+            if t + 1 < PACK:
+                group_max(t + 1)
+            shifted_exp(t)
+        for b in range(2):
+            nc.vector.tensor_reduce(
+                z[:, 2 * b : 2 * b + 2, :].rearrange("p t g -> p (t g)"),
+                p_sb[:, 2 * b : 2 * b + 2, :, :].rearrange("p t g q -> p (t g) q"),
+                AX.X,
+                ALU.add,
+            )
+        log_z = sb("log_z", [P, PACK, G], F32)
+        nc.scalar.activation(log_z[:], z[:], ACT.Ln)
+
+        half_inv = sb("half_inv", [P, PACK], F32)
+        nc.vector.reciprocal(half_inv[:], temp[:])
+        nc.vector.tensor_scalar(half_inv[:], half_inv[:], 0.5, None, ALU.mult)
+        rs_half = sb("rs_half", [P, PACK], F32)
+        nc.vector.tensor_scalar(rs_half[:], rs_sb[:], -0.5, None, ALU.mult)
+
+        half_s = sb("half_s", [P, PACK, G], F32)
+        nc.vector.tensor_tensor(half_s[:], log_z[:], top[:], ALU.add)
+        nc.vector.tensor_tensor(half_s[:], half_s[:], half_inv[:].unsqueeze(2).to_broadcast([P, PACK, G]), ALU.mult)
+        inv_z = sb("inv_z", [P, PACK, G], F32)
+        nc.scalar.activation(inv_z[:], log_z[:], ACT.Exp, scale=-1.0)
+        th = sb("th", [P, PACK, G], F32)
+        nc.scalar.activation(th[:], half_s[:], ACT.Tanh)
+
+        wo_grouped = sb("wo_grouped", [P, PACK, P, PACK], BF16)
+        o, i = dealt_views(wo_grouped, wo_raw, 0, P)
+        nc.vector.tensor_copy(o, i)
+        dy_grouped = sb("dy_grouped", [P, G, PACK], BF16)
+        o, i = plain_views(dy_grouped, dy_raw, 0, G // PACK)
+        nc.vector.tensor_copy(o, i)
+        wo_codes = sb("wo_codes", [P, R], U32)
+        wo_scales = sb("wo_scales", [P, R], U8)
+        nc.vector.quantize_mx(out=wo_codes[:].bitcast(FP8X4), scales=wo_scales[:], in_=wo_grouped[:].rearrange("p t m j -> p (t m j)"))
+        dy_codes = sb("dy_codes", [P, G], U32)
+        dy_scales = sb("dy_scales", [P, G], U8)
+        nc.vector.quantize_mx(out=dy_codes[:].bitcast(FP8X4), scales=dy_scales[:], in_=dy_grouped[:].rearrange("p g j -> p (g j)"))
+
+        c_bank = psum.tile([P, PACK, G], F32, name="c_bank", tag="small")
+        for t in range(PACK):
+            cols = slice(t * P, (t + 1) * P)
+            nc.tensor.matmul_mx(
+                out=c_bank[:, t, :],
+                lhsT=wo_codes[:, cols].bitcast(FP8X4),
+                lhsT_scale=wo_scales[:, cols],
+                rhs=dy_codes[:].bitcast(FP8X4),
+                rhs_scale=dy_scales[:],
+                start=True,
+                stop=True,
+            )
+        c_rs = sb("c_rs", [P, PACK, G], F32)
+        nc.vector.tensor_tensor(c_rs[:], c_bank[:], rs_half[:].unsqueeze(2).to_broadcast([P, PACK, G]), ALU.mult)
+
+        fade_bank = psum.tile([P, P], F32, name="fade_bank", tag="small")
+        nc.tensor.transpose(fade_bank[:], fade_rows[:], ident[:])
+        fade_cols = sb("fade_cols", [P, T // P], F32)
+        nc.scalar.copy(fade_cols[:], fade_bank[:, 0 : T // P])
+
+        w1r_grouped = sb("w1r_grouped", [P, K, PACK], BF16)
+        o, i = plain_views(w1r_grouped, w1r_raw, 0, K // PACK)
+        nc.vector.tensor_copy(o, i)
+        w1r_codes = sb("w1r_codes", [P, K], U32)
+        w1r_scales = sb("w1r_scales", [P, K], U8)
+        nc.vector.quantize_mx(out=w1r_codes[:].bitcast(FP8X4), scales=w1r_scales[:], in_=w1r_grouped[:].rearrange("p c j -> p (c j)"))
+
+        c_z = sb("c_z", [P, PACK, G], F32)
+        nc.vector.tensor_tensor(c_z[:], c_rs[:], inv_z[:], ALU.mult)
+        flat = "p t g -> p (t g)"
+        v = sb("v", [P, PACK * G], F32)
+        nc.vector.scalar_tensor_tensor(v[:], th[:].rearrange(flat), -1.0, half_s[:].rearrange(flat), ALU.add, ALU.mult)
+        u = sb("u", [P, PACK * G], F32)
+        nc.vector.scalar_tensor_tensor(u[:], th[:].rearrange(flat), 1.0, c_z[:].rearrange(flat), ALU.add, ALU.mult)
+        coef = sb("coef", [P, PACK, G], F32)
+        nc.vector.scalar_tensor_tensor(coef[:].rearrange(flat), v[:], -1.0, u[:], ALU.add, ALU.mult)
+
+        gx = [sb(f"gx{a}", [P, J], F32) for a in range(4)]
+        GH = G // 2
+        JH = J // 2
+        for h in range(2):
+            groups = slice(h * GH, (h + 1) * GH)
+            gs = sb(f"gs{h}", [P, GH, POOL, PACK], BF16)
+            nc.vector.tensor_tensor(
+                gs[:].rearrange("p g q t -> p g t q"),
+                p_sb[:, :, groups, :].rearrange("p t g q -> p g t q"),
+                coef[:, :, groups].rearrange("p t g -> p g t").unsqueeze(3).to_broadcast([P, GH, PACK, POOL]),
+                ALU.mult,
+            )
+            gs_codes = sb(f"gs_codes{h}", [P, JH], U32)
+            gs_scales = sb(f"gs_scales{h}", [P, JH], U8)
+            nc.vector.quantize_mx(out=gs_codes[:].bitcast(FP8X4), scales=gs_scales[:], in_=gs[:].rearrange("p g q t -> p (g q t)"))
+            bank = psum.tile([P, 4, JH], F32, name=f"gx_bank{h}", tag=f"mx{h}")
+            for a in range(4):
+                cols = slice(a * P, (a + 1) * P)
+                nc.tensor.matmul_mx(
+                    out=bank[:, a, :],
+                    lhsT=w1r_codes[:, cols].bitcast(FP8X4),
+                    lhsT_scale=w1r_scales[:, cols],
+                    rhs=gs_codes[:].bitcast(FP8X4),
+                    rhs_scale=gs_scales[:],
+                    start=True,
+                    stop=True,
+                )
+            for a in range(4):
+                nc.scalar.copy(gx[a][:, h * JH : (h + 1) * JH], bank[:, a, :])
+
+        faded_t = [sb(f"faded_t{c}", [P, K], F32) for c in range(T // P)]
+        for c in range(T // P):
+            bank = psum.tile([P, K], F32, name=f"turn{c}", tag=f"turn{c % 2}")
+            for a in range(4):
+                nc.tensor.transpose(bank[:, a * P : (a + 1) * P], old_sb[c // 4][:, a, (c % 4) * P : (c % 4 + 1) * P], ident[:])
+            nc.scalar.activation(faded_t[c][:], bank[:], ACT.Copy, scale=fade_cols[:, c : c + 1])
+
+        for h in range(2):
+            nc.vector.tensor_copy(windows[0][:].indirect(offsets[:, 8 * h : 8 * h + 8]), gx[0][:, h * JH : (h + 1) * JH])
+        for a in range(4):
+            if a > 0:
+                nc.vector.tensor_copy(windows[a][:].indirect(offsets[:]), gx[a][:])
+            for h in range(2):
+                bank = psum.tile([P, T // 2], F32, name=f"back{a}_{h}", tag=f"back{(2 * a + h) % 3}")
+                for c in range(4):
+                    nc.tensor.transpose(bank[:, c * P : (c + 1) * P], faded_t[4 * h + c][:, a * P : (a + 1) * P], ident[:])
+                cols = slice(h * (T // 2), (h + 1) * (T // 2))
+                result = sb(f"result{a}_{h}", [P, T // 2], F32)
+                nc.vector.tensor_tensor(result[:], bank[:], windows[a][:, cols], ALU.add)
+                nc.sync.dma_start(out[a * P : (a + 1) * P, cols], result[:])

@@ -23,6 +23,7 @@ PACK = 4
 POOL = J // G
 HALF_M = P // 2
 W1_VECTOR_M = 40
+TURN_BANKS = 5
 
 
 def dealt_views(grouped, raw, m0, m1):
@@ -43,8 +44,8 @@ def tile_attend_csoftmaxpool_x_kernel(tc, tab_words, tab_scales, w1, temper, wo,
         keep = ctx.enter_context(tc.tile_pool(name="keep", bufs=1))
         psum = ctx.enter_context(tc.psum_pool(name="psum", bufs=1))
 
-        def sb(name, shape, dtype):
-            return keep.tile(shape, dtype, name=name, align_bytes=64)
+        def sb(name, shape, dtype, tag=""):
+            return keep.tile(shape, dtype, name=name, align_bytes=64, tag=tag or name)
 
         offsets = keep.tile([P, J // 16], U16, name="offsets")
         nc.sync.dma_start(offsets[:], offs)
@@ -61,12 +62,15 @@ def tile_attend_csoftmaxpool_x_kernel(tc, tab_words, tab_scales, w1, temper, wo,
             raw = sb(f"w1_raw{h}", [P, PACK, R // 2], F32)
             nc.sync.dma_start(raw[:], w1[:, h * (R // 2) : (h + 1) * (R // 2)].rearrange("(p j) c -> p j c", j=PACK))
             w1_raw.append(raw)
-        wo_raw = sb("wo_raw", [P, PACK, R], F32)
-        nc.sync.dma_start(wo_raw[:], wo.rearrange("(p j) c -> p j c", j=PACK))
         temp = sb("temp", [P, PACK], F32)
         nc.sync.dma_start(temp[:], temper.rearrange("(p t) o -> p (t o)", t=PACK))
         dy_raw = sb("dy_raw", [P, PACK, G], F32)
         nc.sync.dma_start(dy_raw[:], dy.rearrange("(p j) c -> p j c", j=PACK))
+        wo_raw = []
+        for h in range(2):
+            raw = sb(f"wo_raw{h}", [P, PACK, R // 2], F32)
+            nc.sync.dma_start(raw[:], wo[:, h * (R // 2) : (h + 1) * (R // 2)].rearrange("(p j) c -> p j c", j=PACK))
+            wo_raw.append(raw)
         w1r_raw = sb("w1r_raw", [P, PACK, K], F32)
         nc.sync.dma_start(w1r_raw[:], w1r.rearrange("(p j) c -> p j c", j=PACK))
         rs_sb = sb("rs_sb", [P, PACK], F32)
@@ -85,7 +89,7 @@ def tile_attend_csoftmaxpool_x_kernel(tc, tab_words, tab_scales, w1, temper, wo,
 
         windows = [keep.tile([P, T], F32, name=f"window{a}") for a in range(4)]
         for a in range(4):
-            (nc.vector if a < 2 else nc.gpsimd).memset(windows[a][:], 0.0)
+            nc.vector.memset(windows[a][:].bitcast(I32), 0)
         for q in range(4):
             nc.vector.tensor_copy(tab_s[32 * q : 32 * q + 4, :].bitcast(I32), scale_rows[32 * q : 32 * q + 4, :])
 
@@ -98,9 +102,11 @@ def tile_attend_csoftmaxpool_x_kernel(tc, tab_words, tab_scales, w1, temper, wo,
         w1_scales = [sb(f"w1_scales{t}", [P, P], U8) for t in range(PACK)]
         for h in range(2):
             grouped = sb(f"w1_grouped{h}", [P, PACK, HALF_M, PACK], BF16)
-            o, i = dealt_views(grouped, w1_raw[h], 0, W1_VECTOR_M)
-            nc.vector.tensor_copy(o, i)
-            o, i = dealt_views(grouped, w1_raw[h], W1_VECTOR_M, HALF_M)
+            split = W1_VECTOR_M if h == 1 else 0
+            if split:
+                o, i = dealt_views(grouped, w1_raw[h], 0, split)
+                nc.vector.tensor_copy(o, i)
+            o, i = dealt_views(grouped, w1_raw[h], split, HALF_M)
             nc.scalar.copy(o, i)
             cols = slice(h * HALF_M, (h + 1) * HALF_M)
             for t in range(PACK):
@@ -134,7 +140,14 @@ def tile_attend_csoftmaxpool_x_kernel(tc, tab_words, tab_scales, w1, temper, wo,
             nc.vector.tensor_reduce(top[:, t, :], x[t][:], AX.X, ALU.max)
 
         def shifted_exp(t):
-            nc.vector.tensor_tensor(below[t][:], x[t][:], top[:, t, :].unsqueeze(2).to_broadcast([P, G, POOL]), ALU.subtract)
+            nc.vector.scalar_tensor_tensor(
+                below[t][:],
+                a_banks[t // 2][:, t % 2, :].rearrange("p (g q) -> p g q", q=POOL),
+                temp[:, t : t + 1],
+                top[:, t, :].unsqueeze(2).to_broadcast([P, G, POOL]),
+                ALU.mult,
+                ALU.subtract,
+            )
             nc.scalar.activation(p_sb[:, t, :, :], below[t][:], ACT.Exp)
 
         group_max(0)
@@ -152,6 +165,25 @@ def tile_attend_csoftmaxpool_x_kernel(tc, tab_words, tab_scales, w1, temper, wo,
         log_z = sb("log_z", [P, PACK, G], F32)
         nc.scalar.activation(log_z[:], z[:], ACT.Ln)
 
+        late_grouped = sb("late_grouped", [P, (R + G) * PACK], BF16, tag="w1_grouped1")
+        dy_grouped = late_grouped[:, R * PACK :].rearrange("p (g j) -> p g j", j=PACK)
+        o, i = plain_views(dy_grouped, dy_raw, 0, G // PACK)
+        nc.vector.tensor_copy(o, i)
+        dy_codes = sb("dy_codes", [P, G], U32)
+        dy_scales = sb("dy_scales", [P, G], U8)
+        nc.vector.quantize_mx(out=dy_codes[:].bitcast(FP8X4), scales=dy_scales[:], in_=late_grouped[:, R * PACK :])
+        wo_grouped = late_grouped[:, : R * PACK].rearrange("p (t m j) -> p t m j", t=PACK, j=PACK)
+        nc.vector.tensor_copy(
+            wo_grouped[:, :, 0:HALF_M, :].rearrange("p t m j -> p m j t"), wo_raw[0][:].rearrange("p j (m t) -> p m j t", t=PACK)
+        )
+        for t in range(PACK):
+            nc.gpsimd.tensor_scalar(
+                wo_grouped[:, t, HALF_M:P, :], wo_raw[1][:].rearrange("p j (m t) -> p t m j", t=PACK)[:, t, :, :], 1.0, 0.0, ALU.mult, ALU.add
+            )
+
+        wo_codes = sb("wo_codes", [P, R], U32)
+        wo_scales = sb("wo_scales", [P, R], U8)
+        nc.vector.quantize_mx(out=wo_codes[:].bitcast(FP8X4), scales=wo_scales[:], in_=late_grouped[:, : R * PACK])
         half_inv = sb("half_inv", [P, PACK], F32)
         nc.vector.reciprocal(half_inv[:], temp[:])
         nc.vector.tensor_scalar(half_inv[:], half_inv[:], 0.5, None, ALU.mult)
@@ -165,19 +197,6 @@ def tile_attend_csoftmaxpool_x_kernel(tc, tab_words, tab_scales, w1, temper, wo,
         nc.scalar.activation(inv_z[:], log_z[:], ACT.Exp, scale=-1.0)
         th = sb("th", [P, PACK, G], F32)
         nc.scalar.activation(th[:], half_s[:], ACT.Tanh)
-
-        wo_grouped = sb("wo_grouped", [P, PACK, P, PACK], BF16)
-        o, i = dealt_views(wo_grouped, wo_raw, 0, P)
-        nc.vector.tensor_copy(o, i)
-        dy_grouped = sb("dy_grouped", [P, G, PACK], BF16)
-        o, i = plain_views(dy_grouped, dy_raw, 0, G // PACK)
-        nc.vector.tensor_copy(o, i)
-        wo_codes = sb("wo_codes", [P, R], U32)
-        wo_scales = sb("wo_scales", [P, R], U8)
-        nc.vector.quantize_mx(out=wo_codes[:].bitcast(FP8X4), scales=wo_scales[:], in_=wo_grouped[:].rearrange("p t m j -> p (t m j)"))
-        dy_codes = sb("dy_codes", [P, G], U32)
-        dy_scales = sb("dy_scales", [P, G], U8)
-        nc.vector.quantize_mx(out=dy_codes[:].bitcast(FP8X4), scales=dy_scales[:], in_=dy_grouped[:].rearrange("p g j -> p (g j)"))
 
         c_bank = psum.tile([P, PACK, G], F32, name="c_bank", tag="small")
         for t in range(PACK):
@@ -194,7 +213,7 @@ def tile_attend_csoftmaxpool_x_kernel(tc, tab_words, tab_scales, w1, temper, wo,
         c_rs = sb("c_rs", [P, PACK, G], F32)
         nc.vector.tensor_tensor(c_rs[:], c_bank[:], rs_half[:].unsqueeze(2).to_broadcast([P, PACK, G]), ALU.mult)
 
-        fade_bank = psum.tile([P, P], F32, name="fade_bank", tag="small")
+        fade_bank = psum.tile([P, P], F32, name="fade_bank", tag="turn", bufs=TURN_BANKS)
         nc.tensor.transpose(fade_bank[:], fade_rows[:], ident[:])
         fade_cols = sb("fade_cols", [P, T // P], F32)
         nc.scalar.copy(fade_cols[:], fade_bank[:, 0 : T // P])
@@ -216,7 +235,7 @@ def tile_attend_csoftmaxpool_x_kernel(tc, tab_words, tab_scales, w1, temper, wo,
         coef = sb("coef", [P, PACK, G], F32)
         nc.vector.scalar_tensor_tensor(coef[:].rearrange(flat), v[:], -1.0, u[:], ALU.add, ALU.mult)
 
-        gx = [sb(f"gx{a}", [P, J], F32) for a in range(4)]
+        gx = sb("gx", [P, 4, J], F32)
         GH = G // 2
         JH = J // 2
         for h in range(2):
@@ -231,11 +250,19 @@ def tile_attend_csoftmaxpool_x_kernel(tc, tab_words, tab_scales, w1, temper, wo,
             gs_codes = sb(f"gs_codes{h}", [P, JH], U32)
             gs_scales = sb(f"gs_scales{h}", [P, JH], U8)
             nc.vector.quantize_mx(out=gs_codes[:].bitcast(FP8X4), scales=gs_scales[:], in_=gs[:].rearrange("p g q t -> p (g q t)"))
-            bank = psum.tile([P, 4, JH], F32, name=f"gx_bank{h}", tag=f"mx{h}")
+            if h == 0:
+                first = psum.tile([P, 1, JH], F32, name="gx_first", tag="mx0")
+                rest = psum.tile([P, 3, JH], F32, name="gx_rest", tag="mx1")
+                places = [first[:, 0, :]] + [rest[:, a, :] for a in range(3)]
+                parts = [(slice(0, 1), first[:]), (slice(1, 4), rest[:])]
+            else:
+                bank = psum.tile([P, 4, JH], F32, name="gx_late", tag="small")
+                places = [bank[:, a, :] for a in range(4)]
+                parts = [(slice(0, 2), bank[:, 0:2, :]), (slice(2, 4), bank[:, 2:4, :])]
             for a in range(4):
                 cols = slice(a * P, (a + 1) * P)
                 nc.tensor.matmul_mx(
-                    out=bank[:, a, :],
+                    out=places[a],
                     lhsT=w1r_codes[:, cols].bitcast(FP8X4),
                     lhsT_scale=w1r_scales[:, cols],
                     rhs=gs_codes[:].bitcast(FP8X4),
@@ -243,26 +270,54 @@ def tile_attend_csoftmaxpool_x_kernel(tc, tab_words, tab_scales, w1, temper, wo,
                     start=True,
                     stop=True,
                 )
-            for a in range(4):
-                nc.scalar.copy(gx[a][:, h * JH : (h + 1) * JH], bank[:, a, :])
+            slots = slice(h * JH, (h + 1) * JH)
+            for tiles, source in parts:
+                nc.scalar.copy(gx[:, tiles, slots], source)
 
         faded_t = [sb(f"faded_t{c}", [P, K], F32) for c in range(T // P)]
-        for c in range(T // P):
-            bank = psum.tile([P, K], F32, name=f"turn{c}", tag=f"turn{c % 2}")
+
+        def fade_chunk(c):
+            bank = psum.tile([P, K], F32, name=f"turn{c}", tag="turn", bufs=TURN_BANKS)
             for a in range(4):
                 nc.tensor.transpose(bank[:, a * P : (a + 1) * P], old_sb[c // 4][:, a, (c % 4) * P : (c % 4 + 1) * P], ident[:])
             nc.scalar.activation(faded_t[c][:], bank[:], ACT.Copy, scale=fade_cols[:, c : c + 1])
 
-        for h in range(2):
-            nc.vector.tensor_copy(windows[0][:].indirect(offsets[:, 8 * h : 8 * h + 8]), gx[0][:, h * JH : (h + 1) * JH])
-        for a in range(4):
-            if a > 0:
-                nc.vector.tensor_copy(windows[a][:].indirect(offsets[:]), gx[a][:])
-            for h in range(2):
-                bank = psum.tile([P, T // 2], F32, name=f"back{a}_{h}", tag=f"back{(2 * a + h) % 3}")
-                for c in range(4):
-                    nc.tensor.transpose(bank[:, c * P : (c + 1) * P], faded_t[4 * h + c][:, a * P : (a + 1) * P], ident[:])
-                cols = slice(h * (T // 2), (h + 1) * (T // 2))
-                result = sb(f"result{a}_{h}", [P, T // 2], F32)
-                nc.vector.tensor_tensor(result[:], bank[:], windows[a][:, cols], ALU.add)
-                nc.sync.dma_start(out[a * P : (a + 1) * P, cols], result[:])
+        def turn_back(a, h, tag, bufs=1):
+            bank = psum.tile([P, T // 2], F32, name=f"back{a}_{h}", tag=tag, bufs=bufs)
+            for c in range(4):
+                nc.tensor.transpose(bank[:, c * P : (c + 1) * P], faded_t[4 * h + c][:, a * P : (a + 1) * P], ident[:])
+            return bank
+
+        def finish(a, h, engine, faded, tag=""):
+            cols = slice(h * (T // 2), (h + 1) * (T // 2))
+            result = sb(f"result{a}_{h}", [P, T // 2], F32, tag)
+            engine.tensor_tensor(result[:], faded[:], windows[a][:, cols], ALU.add)
+            nc.sync.dma_start(out[a * P : (a + 1) * P, cols], result[:])
+
+        def finish_on_gpsimd(a, h):
+            bank = turn_back(a, h, "turn", TURN_BANKS)
+            faded = sb(f"faded{a}_{h}", [P, T // 2], F32)
+            nc.scalar.copy(faded[:], bank[:])
+            finish(a, h, nc.gpsimd, faded)
+
+        def scatter(a, h0, h1):
+            nc.vector.tensor_copy(windows[a][:].indirect(offsets[:, 8 * h0 : 8 * h1]), gx[:, a, h0 * JH : h1 * JH])
+
+        scatter(0, 0, 1)
+        scatter(1, 0, 1)
+        scatter(0, 1, 2)
+        scatter(1, 1, 2)
+        scatter(2, 0, 2)
+        for c in range(4):
+            fade_chunk(c)
+        finish_on_gpsimd(0, 0)
+        for c in range(4, 8):
+            fade_chunk(c)
+        finish_on_gpsimd(0, 1)
+        finish_on_gpsimd(1, 0)
+        finish_on_gpsimd(1, 1)
+        finish_on_gpsimd(2, 0)
+        finish(2, 1, nc.vector, turn_back(2, 1, "mx0"), "faded0_1")
+        scatter(3, 0, 2)
+        finish(3, 0, nc.vector, turn_back(3, 0, "mx1"), "faded1_1")
+        finish(3, 1, nc.vector, turn_back(3, 1, "small"))

@@ -27,8 +27,8 @@ TURN_BANKS = 5
 
 
 def dealt_views(grouped, raw, m0, m1):
-    out = grouped[:, :, m0:m1, :].rearrange("p t m j -> p m j t")
-    in_ = raw[:].rearrange("p j (m t) -> p m j t", t=PACK)[:, m0:m1, :, :]
+    out = grouped[:, :, m0:m1, :].rearrange("p t (n e) j -> p n j e t", e=2)
+    in_ = raw[:, :, m0 * PACK : m1 * PACK].rearrange("p j (n e t) -> p n j e t", e=2, t=PACK)
     return out, in_
 
 
@@ -83,12 +83,16 @@ def tile_attend_csoftmaxpool_x_kernel(tc, tab_words, tab_scales, w1, temper, wo,
             tile = sb(f"old{h}", [P, 4, T // 2], F32)
             nc.sync.dma_start(tile[:], old[:, h * (T // 2) : (h + 1) * (T // 2)].rearrange("(a p) c -> p a c", p=P))
             old_sb.append(tile)
+        fade_wide = sb("fade_wide", [P, T // 2], F32)
+        nc.sync.dma_start(fade_wide[:], fade[0, 0 : T // 2].partition_broadcast(P))
 
         ident = sb("ident", [P, P], F32)
         make_identity(nc, ident[:])
+        one_half = sb("one_half", [P, 1], F32)
+        nc.gpsimd.memset(one_half[:], 0.5)
 
-        windows = [keep.tile([P, T], F32, name=f"window{a}") for a in range(4)]
-        for a in range(4):
+        windows = [sb(f"window{a}", [P, T], F32) for a in range(2)]
+        for a in range(2):
             nc.vector.memset(windows[a][:].bitcast(I32), 0)
         for q in range(4):
             nc.vector.tensor_copy(tab_s[32 * q : 32 * q + 4, :].bitcast(I32), scale_rows[32 * q : 32 * q + 4, :])
@@ -134,20 +138,14 @@ def tile_attend_csoftmaxpool_x_kernel(tc, tab_words, tab_scales, w1, temper, wo,
         top = sb("top", [P, PACK, G], F32)
         below = [sb(f"below{t}", [P, G, POOL], F32) for t in range(PACK)]
         p_sb = sb("p_sb", [P, PACK, G, POOL], F32)
-        z = sb("z", [P, PACK, G], F32)
 
         def group_max(t):
             nc.vector.tensor_reduce(top[:, t, :], x[t][:], AX.X, ALU.max)
 
         def shifted_exp(t):
-            nc.vector.scalar_tensor_tensor(
-                below[t][:],
-                a_banks[t // 2][:, t % 2, :].rearrange("p (g q) -> p g q", q=POOL),
-                temp[:, t : t + 1],
-                top[:, t, :].unsqueeze(2).to_broadcast([P, G, POOL]),
-                ALU.mult,
-                ALU.subtract,
-            )
+            spread = top[:, t, :].unsqueeze(2).to_broadcast([P, G, POOL])
+            sums = a_banks[t // 2][:, t % 2, :].rearrange("p (g q) -> p g q", q=POOL)
+            nc.vector.scalar_tensor_tensor(below[t][:], sums, temp[:, t : t + 1], spread, ALU.mult, ALU.subtract)
             nc.scalar.activation(p_sb[:, t, :, :], below[t][:], ACT.Exp)
 
         group_max(0)
@@ -155,15 +153,19 @@ def tile_attend_csoftmaxpool_x_kernel(tc, tab_words, tab_scales, w1, temper, wo,
             if t + 1 < PACK:
                 group_max(t + 1)
             shifted_exp(t)
+        z_bank = psum.tile([P, 2, P], F32, name="z_bank", tag="turn", bufs=TURN_BANKS)
         for b in range(2):
-            nc.vector.tensor_reduce(
-                z[:, 2 * b : 2 * b + 2, :].rearrange("p t g -> p (t g)"),
-                p_sb[:, 2 * b : 2 * b + 2, :, :].rearrange("p t g q -> p (t g) q"),
-                AX.X,
-                ALU.add,
-            )
-        log_z = sb("log_z", [P, PACK, G], F32)
-        nc.scalar.activation(log_z[:], z[:], ACT.Ln)
+            pooled = p_sb[:, 2 * b : 2 * b + 2, :, :].rearrange("p t g q -> p (t g) q")
+            for q in range(POOL):
+                nc.tensor.matmul(z_bank[:, b, :], pooled[:, :, q], ident[:], start=(q == 0), stop=(q == POOL - 1), is_transpose=True)
+        log_z_turned = sb("log_z_turned", [P, 2, P], F32)
+        nc.scalar.activation(log_z_turned[:], z_bank[:], ACT.Ln)
+        log_z = []
+        for reader in range(2):
+            bank = psum.tile([P, PACK, G], F32, name=f"log_z{reader}", tag="turn", bufs=TURN_BANKS)
+            for b in range(2):
+                nc.tensor.transpose(bank[:, 2 * b : 2 * b + 2, :].rearrange("p t g -> p (t g)"), log_z_turned[:, b, :], ident[:])
+            log_z.append(bank)
 
         late_grouped = sb("late_grouped", [P, (R + G) * PACK], BF16, tag="w1_grouped1")
         dy_grouped = late_grouped[:, R * PACK :].rearrange("p (g j) -> p g j", j=PACK)
@@ -173,9 +175,8 @@ def tile_attend_csoftmaxpool_x_kernel(tc, tab_words, tab_scales, w1, temper, wo,
         dy_scales = sb("dy_scales", [P, G], U8)
         nc.vector.quantize_mx(out=dy_codes[:].bitcast(FP8X4), scales=dy_scales[:], in_=late_grouped[:, R * PACK :])
         wo_grouped = late_grouped[:, : R * PACK].rearrange("p (t m j) -> p t m j", t=PACK, j=PACK)
-        nc.vector.tensor_copy(
-            wo_grouped[:, :, 0:HALF_M, :].rearrange("p t m j -> p m j t"), wo_raw[0][:].rearrange("p j (m t) -> p m j t", t=PACK)
-        )
+        o, i = dealt_views(wo_grouped, wo_raw[0], 0, HALF_M)
+        nc.vector.tensor_copy(o, i)
         for t in range(PACK):
             nc.gpsimd.tensor_scalar(
                 wo_grouped[:, t, HALF_M:P, :], wo_raw[1][:].rearrange("p j (m t) -> p t m j", t=PACK)[:, t, :, :], 1.0, 0.0, ALU.mult, ALU.add
@@ -186,17 +187,16 @@ def tile_attend_csoftmaxpool_x_kernel(tc, tab_words, tab_scales, w1, temper, wo,
         nc.vector.quantize_mx(out=wo_codes[:].bitcast(FP8X4), scales=wo_scales[:], in_=late_grouped[:, : R * PACK])
         half_inv = sb("half_inv", [P, PACK], F32)
         nc.vector.reciprocal(half_inv[:], temp[:])
-        nc.vector.tensor_scalar(half_inv[:], half_inv[:], 0.5, None, ALU.mult)
-        rs_half = sb("rs_half", [P, PACK], F32)
-        nc.vector.tensor_scalar(rs_half[:], rs_sb[:], -0.5, None, ALU.mult)
 
         half_s = sb("half_s", [P, PACK, G], F32)
-        nc.vector.tensor_tensor(half_s[:], log_z[:], top[:], ALU.add)
+        nc.vector.tensor_tensor(half_s[:], log_z[0][:], top[:], ALU.add)
         nc.vector.tensor_tensor(half_s[:], half_s[:], half_inv[:].unsqueeze(2).to_broadcast([P, PACK, G]), ALU.mult)
         inv_z = sb("inv_z", [P, PACK, G], F32)
-        nc.scalar.activation(inv_z[:], log_z[:], ACT.Exp, scale=-1.0)
+        nc.scalar.activation(inv_z[:], log_z[1][:], ACT.Exp, scale=-1.0)
         th = sb("th", [P, PACK, G], F32)
-        nc.scalar.activation(th[:], half_s[:], ACT.Tanh)
+        for h in range(2):
+            groups = slice(h * (G // 2), (h + 1) * (G // 2))
+            nc.scalar.activation(th[:, :, groups], half_s[:, :, groups], ACT.Tanh, scale=one_half[:])
 
         c_bank = psum.tile([P, PACK, G], F32, name="c_bank", tag="small")
         for t in range(PACK):
@@ -211,11 +211,11 @@ def tile_attend_csoftmaxpool_x_kernel(tc, tab_words, tab_scales, w1, temper, wo,
                 stop=True,
             )
         c_rs = sb("c_rs", [P, PACK, G], F32)
-        nc.vector.tensor_tensor(c_rs[:], c_bank[:], rs_half[:].unsqueeze(2).to_broadcast([P, PACK, G]), ALU.mult)
+        nc.vector.scalar_tensor_tensor(c_rs[:], c_bank[:], -0.25, rs_sb[:].unsqueeze(2).to_broadcast([P, PACK, G]), ALU.mult, ALU.mult)
 
         fade_bank = psum.tile([P, P], F32, name="fade_bank", tag="turn", bufs=TURN_BANKS)
         nc.tensor.transpose(fade_bank[:], fade_rows[:], ident[:])
-        fade_cols = sb("fade_cols", [P, T // P], F32)
+        fade_cols = sb("fade_cols", [P, T // P], F32, "one_half")
         nc.scalar.copy(fade_cols[:], fade_bank[:, 0 : T // P])
 
         w1r_grouped = sb("w1r_grouped", [P, K, PACK], BF16)
@@ -223,46 +223,49 @@ def tile_attend_csoftmaxpool_x_kernel(tc, tab_words, tab_scales, w1, temper, wo,
         nc.vector.tensor_copy(o, i)
         w1r_codes = sb("w1r_codes", [P, K], U32)
         w1r_scales = sb("w1r_scales", [P, K], U8)
-        nc.vector.quantize_mx(out=w1r_codes[:].bitcast(FP8X4), scales=w1r_scales[:], in_=w1r_grouped[:].rearrange("p c j -> p (c j)"))
+
+        def quantize_w1r(a):
+            cols = slice(a * P, (a + 1) * P)
+            nc.vector.quantize_mx(
+                out=w1r_codes[:, cols].bitcast(FP8X4), scales=w1r_scales[:, cols], in_=w1r_grouped[:, cols, :].rearrange("p c j -> p (c j)")
+            )
+
+        for a in range(4):
+            quantize_w1r(a)
 
         c_z = sb("c_z", [P, PACK, G], F32)
         nc.vector.tensor_tensor(c_z[:], c_rs[:], inv_z[:], ALU.mult)
-        flat = "p t g -> p (t g)"
-        v = sb("v", [P, PACK * G], F32)
-        nc.vector.scalar_tensor_tensor(v[:], th[:].rearrange(flat), -1.0, half_s[:].rearrange(flat), ALU.add, ALU.mult)
-        u = sb("u", [P, PACK * G], F32)
-        nc.vector.scalar_tensor_tensor(u[:], th[:].rearrange(flat), 1.0, c_z[:].rearrange(flat), ALU.add, ALU.mult)
-        coef = sb("coef", [P, PACK, G], F32)
-        nc.vector.scalar_tensor_tensor(coef[:].rearrange(flat), v[:], -1.0, u[:], ALU.add, ALU.mult)
-
         gx = sb("gx", [P, 4, J], F32)
         GH = G // 2
         JH = J // 2
         for h in range(2):
             groups = slice(h * GH, (h + 1) * GH)
+            v = sb(f"v{h}", [P, PACK, GH], F32)
+            nc.vector.scalar_tensor_tensor(v[:], th[:, :, groups], -1.0, half_s[:, :, groups], ALU.add, ALU.mult)
+            u = sb(f"u{h}", [P, PACK, GH], F32)
+            nc.vector.scalar_tensor_tensor(u[:], th[:, :, groups], 1.0, c_z[:, :, groups], ALU.add, ALU.mult)
+            coef = sb(f"coef{h}", [P, PACK, GH], F32)
+            nc.vector.scalar_tensor_tensor(coef[:], v[:], -2.0, u[:], ALU.add, ALU.mult)
             gs = sb(f"gs{h}", [P, GH, POOL, PACK], BF16)
             nc.vector.tensor_tensor(
                 gs[:].rearrange("p g q t -> p g t q"),
                 p_sb[:, :, groups, :].rearrange("p t g q -> p g t q"),
-                coef[:, :, groups].rearrange("p t g -> p g t").unsqueeze(3).to_broadcast([P, GH, PACK, POOL]),
+                coef[:].rearrange("p t g -> p g t").unsqueeze(3).to_broadcast([P, GH, PACK, POOL]),
                 ALU.mult,
             )
             gs_codes = sb(f"gs_codes{h}", [P, JH], U32)
             gs_scales = sb(f"gs_scales{h}", [P, JH], U8)
             nc.vector.quantize_mx(out=gs_codes[:].bitcast(FP8X4), scales=gs_scales[:], in_=gs[:].rearrange("p g q t -> p (g q t)"))
             if h == 0:
-                first = psum.tile([P, 1, JH], F32, name="gx_first", tag="mx0")
-                rest = psum.tile([P, 3, JH], F32, name="gx_rest", tag="mx1")
-                places = [first[:, 0, :]] + [rest[:, a, :] for a in range(3)]
-                parts = [(slice(0, 1), first[:]), (slice(1, 4), rest[:])]
+                first = psum.tile([P, 1, JH], F32, name="gx_first0", tag="mx0")
+                rest = psum.tile([P, 3, JH], F32, name="gx_rest0", tag="mx1")
             else:
-                bank = psum.tile([P, 4, JH], F32, name="gx_late", tag="small")
-                places = [bank[:, a, :] for a in range(4)]
-                parts = [(slice(0, 2), bank[:, 0:2, :]), (slice(2, 4), bank[:, 2:4, :])]
+                first = psum.tile([P, 1, JH], F32, name="gx_first1", tag="small")
+                rest = psum.tile([P, 3, JH], F32, name="gx_rest1", tag="mx0")
             for a in range(4):
                 cols = slice(a * P, (a + 1) * P)
                 nc.tensor.matmul_mx(
-                    out=places[a],
+                    out=first[:, 0, :] if a == 0 else rest[:, a - 1, :],
                     lhsT=w1r_codes[:, cols].bitcast(FP8X4),
                     lhsT_scale=w1r_scales[:, cols],
                     rhs=gs_codes[:].bitcast(FP8X4),
@@ -271,16 +274,22 @@ def tile_attend_csoftmaxpool_x_kernel(tc, tab_words, tab_scales, w1, temper, wo,
                     stop=True,
                 )
             slots = slice(h * JH, (h + 1) * JH)
-            for tiles, source in parts:
-                nc.scalar.copy(gx[:, tiles, slots], source)
+            nc.scalar.copy(gx[:, 0:1, slots], first[:])
+            nc.scalar.copy(gx[:, 1:4, slots], rest[:])
+
+        for a, tag in ((2, "gs0"), (3, "gs_codes1")):
+            windows.append(sb(f"window{a}", [P, T], F32, tag))
+            nc.gpsimd.memset(windows[a][:], 0.0)
 
         faded_t = [sb(f"faded_t{c}", [P, K], F32) for c in range(T // P)]
 
         def fade_chunk(c):
             bank = psum.tile([P, K], F32, name=f"turn{c}", tag="turn", bufs=TURN_BANKS)
-            for a in range(4):
+            first_tile = 1 if c < 4 else 0
+            for a in range(first_tile, 4):
                 nc.tensor.transpose(bank[:, a * P : (a + 1) * P], old_sb[c // 4][:, a, (c % 4) * P : (c % 4 + 1) * P], ident[:])
-            nc.scalar.activation(faded_t[c][:], bank[:], ACT.Copy, scale=fade_cols[:, c : c + 1])
+            rows = slice(first_tile * P, K)
+            nc.scalar.activation(faded_t[c][:, rows], bank[:, rows], ACT.Copy, scale=fade_cols[:, c : c + 1])
 
         def turn_back(a, h, tag, bufs=1):
             bank = psum.tile([P, T // 2], F32, name=f"back{a}_{h}", tag=tag, bufs=bufs)
@@ -288,36 +297,40 @@ def tile_attend_csoftmaxpool_x_kernel(tc, tab_words, tab_scales, w1, temper, wo,
                 nc.tensor.transpose(bank[:, c * P : (c + 1) * P], faded_t[4 * h + c][:, a * P : (a + 1) * P], ident[:])
             return bank
 
-        def finish(a, h, engine, faded, tag=""):
-            cols = slice(h * (T // 2), (h + 1) * (T // 2))
-            result = sb(f"result{a}_{h}", [P, T // 2], F32, tag)
-            engine.tensor_tensor(result[:], faded[:], windows[a][:, cols], ALU.add)
-            nc.sync.dma_start(out[a * P : (a + 1) * P, cols], result[:])
+        def finish(a, c0, c1, engine, faded, tag=""):
+            result = sb(f"result{a}_{c0}", [P, c1 - c0], F32, tag)
+            engine.tensor_tensor(result[:], faded, windows[a][:, c0:c1], ALU.add)
+            nc.sync.dma_start(out[a * P : (a + 1) * P, c0:c1], result[:])
 
-        def finish_on_gpsimd(a, h):
-            bank = turn_back(a, h, "turn", TURN_BANKS)
-            faded = sb(f"faded{a}_{h}", [P, T // 2], F32)
-            nc.scalar.copy(faded[:], bank[:])
-            finish(a, h, nc.gpsimd, faded)
+        def finish_on_gpsimd(a, c0, c1, source):
+            faded = sb(f"faded{a}_{c0}", [P, c1 - c0], F32)
+            nc.scalar.copy(faded[:], source)
+            finish(a, c0, c1, nc.gpsimd, faded[:])
 
         def scatter(a, h0, h1):
             nc.vector.tensor_copy(windows[a][:].indirect(offsets[:, 8 * h0 : 8 * h1]), gx[:, a, h0 * JH : h1 * JH])
 
+        H, Q = T // 2, T // 4
         scatter(0, 0, 1)
-        scatter(1, 0, 1)
         scatter(0, 1, 2)
-        scatter(1, 1, 2)
+        scatter(1, 0, 2)
         scatter(2, 0, 2)
         for c in range(4):
             fade_chunk(c)
-        finish_on_gpsimd(0, 0)
+        faded = sb("faded0_0", [P, H], F32, "gs1")
+        nc.gpsimd.tensor_tensor(faded[:], old_sb[0][:, 0, :], fade_wide[:], ALU.mult)
+        finish(0, 0, H, nc.gpsimd, faded[:])
         for c in range(4, 8):
             fade_chunk(c)
-        finish_on_gpsimd(0, 1)
-        finish_on_gpsimd(1, 0)
-        finish_on_gpsimd(1, 1)
-        finish_on_gpsimd(2, 0)
-        finish(2, 1, nc.vector, turn_back(2, 1, "mx0"), "faded0_1")
+        finish_on_gpsimd(1, 0, H, turn_back(1, 0, "small")[:])
+        finish_on_gpsimd(0, H, T, turn_back(0, 1, "turn", TURN_BANKS)[:])
+        finish_on_gpsimd(1, H, T, turn_back(1, 1, "turn", TURN_BANKS)[:])
+        bank = turn_back(2, 0, "mx1")
+        finish_on_gpsimd(2, 0, Q, bank[:, 0:Q])
+        finish(2, Q, H, nc.vector, bank[:, Q:H], "faded1_0")
+        finish(2, H, T, nc.vector, turn_back(2, 1, "small")[:])
         scatter(3, 0, 2)
-        finish(3, 0, nc.vector, turn_back(3, 0, "mx1"), "faded1_1")
-        finish(3, 1, nc.vector, turn_back(3, 1, "small"))
+        finish(3, 0, H, nc.vector, turn_back(3, 0, "mx0")[:], "faded1_512")
+        bank = turn_back(3, 1, "turn", TURN_BANKS)
+        finish(3, H, H + Q, nc.vector, bank[:, 0:Q])
+        finish(3, H + Q, T, nc.vector, bank[:, Q:H])

@@ -21,20 +21,28 @@ AX = mybir.AxisListType
 P = 128
 PACK = 4
 POOL = J // G
+K_TILES = K // P
+CHUNKS = T // P
+QUADRANT = 32
+LIST_ROWS = 16
 HALF_M = P // 2
-W1_VECTOR_M = 40
+HALF_R = R // 2
+HALF_G = G // 2
+HALF_J = J // 2
+HALF_T = T // 2
+QUARTER_T = T // 4
 TURN_BANKS = 5
 
 
-def dealt_views(grouped, raw, m0, m1):
-    out = grouped[:, :, m0:m1, :].rearrange("p t (n e) j -> p n j e t", e=2)
-    in_ = raw[:, :, m0 * PACK : m1 * PACK].rearrange("p j (n e t) -> p n j e t", e=2, t=PACK)
+def dealt_views(grouped, raw, t0, t1):
+    out = grouped[:, t0:t1, :, :].rearrange("p t (n e) j -> p n j e t", e=2)
+    in_ = raw[:].rearrange("p j (n e t) -> p n j e t", e=2, t=PACK)[:, :, :, :, t0:t1]
     return out, in_
 
 
-def plain_views(grouped, raw, c0, c1):
-    out = grouped[:].rearrange("p (c i) j -> p c j i", i=PACK)[:, c0:c1, :, :]
-    in_ = raw[:].rearrange("p j (c i) -> p c j i", i=PACK)[:, c0:c1, :, :]
+def interleaved_views(grouped, raw):
+    out = grouped.rearrange("p (n i) j -> p n j i", i=PACK)
+    in_ = raw.rearrange("p j (n i) -> p n j i", i=PACK)
     return out, in_
 
 
@@ -44,58 +52,63 @@ def tile_attend_csoftmaxpool_x_kernel(tc, tab_words, tab_scales, w1, temper, wo,
         keep = ctx.enter_context(tc.tile_pool(name="keep", bufs=1))
         psum = ctx.enter_context(tc.psum_pool(name="psum", bufs=1))
 
-        def sb(name, shape, dtype, tag=""):
-            return keep.tile(shape, dtype, name=name, align_bytes=64, tag=tag or name)
+        def sb(name, shape, dtype, reuse=""):
+            return keep.tile(shape, dtype, name=name, align_bytes=64, tag=reuse or name)
 
-        offsets = keep.tile([P, J // 16], U16, name="offsets")
+        def turn_bank(name, shape):
+            return psum.tile(shape, F32, name=name, tag="turn", bufs=TURN_BANKS)
+
+        def product(out_ap, codes, scales, moving_codes, moving_scales):
+            nc.tensor.matmul_mx(
+                out=out_ap, lhsT=codes.bitcast(FP8X4), lhsT_scale=scales, rhs=moving_codes, rhs_scale=moving_scales, start=True, stop=True
+            )
+
+        offsets = keep.tile([P, J // LIST_ROWS], U16, name="offsets")
         nc.sync.dma_start(offsets[:], offs)
-
         tab_s = sb("tab_s", [P, T], U8)
         nc.vector.memset(tab_s[:].bitcast(I32), 0)
         scale_rows = sb("scale_rows", [P, T // 4], I32)
-        for q in range(4):
-            nc.scalar.dma_start(scale_rows[32 * q : 32 * q + 4, :], tab_scales[0, 4 * q : 4 * q + 4, :].bitcast(I32))
+        live_rows = [slice(QUADRANT * q, QUADRANT * q + 4) for q in range(P // QUADRANT)]
+        for q, rows in enumerate(live_rows):
+            nc.scalar.dma_start(scale_rows[rows, :], tab_scales[0, 4 * q : 4 * q + 4, :].bitcast(I32))
         tab_w = sb("tab_w", [P, T], U16)
         nc.sync.dma_start(tab_w[:].bitcast(I32), tab_words[0].bitcast(I32))
-        w1_raw = []
-        for h in range(2):
-            raw = sb(f"w1_raw{h}", [P, PACK, R // 2], F32)
-            nc.sync.dma_start(raw[:], w1[:, h * (R // 2) : (h + 1) * (R // 2)].rearrange("(p j) c -> p j c", j=PACK))
-            w1_raw.append(raw)
-        temp = sb("temp", [P, PACK], F32)
-        nc.sync.dma_start(temp[:], temper.rearrange("(p t) o -> p (t o)", t=PACK))
-        dy_raw = sb("dy_raw", [P, PACK, G], F32)
-        nc.sync.dma_start(dy_raw[:], dy.rearrange("(p j) c -> p j c", j=PACK))
-        wo_raw = []
-        for h in range(2):
-            raw = sb(f"wo_raw{h}", [P, PACK, R // 2], F32)
-            nc.sync.dma_start(raw[:], wo[:, h * (R // 2) : (h + 1) * (R // 2)].rearrange("(p j) c -> p j c", j=PACK))
-            wo_raw.append(raw)
-        w1r_raw = sb("w1r_raw", [P, PACK, K], F32)
-        nc.sync.dma_start(w1r_raw[:], w1r.rearrange("(p j) c -> p j c", j=PACK))
-        rs_sb = sb("rs_sb", [P, PACK], F32)
-        nc.sync.dma_start(rs_sb[:], rs.rearrange("(p t) o -> p (t o)", t=PACK))
+
+        def load_rows(name, source):
+            raw = sb(name, [P, PACK, source.shape[1]], F32)
+            nc.sync.dma_start(raw[:], source.rearrange("(p j) c -> p j c", j=PACK))
+            return raw
+
+        def load_by_feature(name, source):
+            tile = sb(name, [P, PACK], F32)
+            nc.sync.dma_start(tile[:], source.rearrange("(p t) o -> p (t o)", t=PACK))
+            return tile
+
+        w1_raw = [load_rows(f"w1_raw{h}", w1[:, h * HALF_R : (h + 1) * HALF_R]) for h in range(2)]
+        temper_sb = load_by_feature("temper_sb", temper)
+        dy_raw = load_rows("dy_raw", dy)
+        wo_raw = [load_rows(f"wo_raw{h}", wo[:, h * HALF_R : (h + 1) * HALF_R]) for h in range(2)]
+        w1r_raw = load_rows("w1r_raw", w1r)
+        rs_sb = load_by_feature("rs_sb", rs)
         fade_rows = sb("fade_rows", [P, P], F32)
         nc.gpsimd.memset(fade_rows[:], 0.0)
-        nc.sync.dma_start(fade_rows[0 : T // P, :], fade.rearrange("o (c p) -> (o c) p", p=P))
+        nc.sync.dma_start(fade_rows[0:CHUNKS, :], fade.rearrange("o (c p) -> (o c) p", p=P))
         old_sb = []
         for h in range(2):
-            tile = sb(f"old{h}", [P, 4, T // 2], F32)
-            nc.sync.dma_start(tile[:], old[:, h * (T // 2) : (h + 1) * (T // 2)].rearrange("(a p) c -> p a c", p=P))
-            old_sb.append(tile)
-        fade_wide = sb("fade_wide", [P, T // 2], F32)
-        nc.sync.dma_start(fade_wide[:], fade[0, 0 : T // 2].partition_broadcast(P))
+            old_half = sb(f"old{h}", [P, K_TILES, HALF_T], F32)
+            nc.sync.dma_start(old_half[:], old[:, h * HALF_T : (h + 1) * HALF_T].rearrange("(a p) c -> p a c", p=P))
+            old_sb.append(old_half)
 
         ident = sb("ident", [P, P], F32)
         make_identity(nc, ident[:])
         one_half = sb("one_half", [P, 1], F32)
         nc.gpsimd.memset(one_half[:], 0.5)
 
-        windows = [sb(f"window{a}", [P, T], F32) for a in range(2)]
-        for a in range(2):
-            nc.vector.memset(windows[a][:].bitcast(I32), 0)
-        for q in range(4):
-            nc.vector.tensor_copy(tab_s[32 * q : 32 * q + 4, :].bitcast(I32), scale_rows[32 * q : 32 * q + 4, :])
+        windows = [sb(f"window{a}", [P, T], F32) for a in range(K_TILES)]
+        for window in windows:
+            nc.vector.memset(window[:].bitcast(I32), 0)
+        for rows in live_rows:
+            nc.vector.tensor_copy(tab_s[rows, :].bitcast(I32), scale_rows[rows, :])
 
         got_w = sb("got_w", [P, J], U16)
         nc.vector.tensor_copy(got_w[:], tab_w[:].indirect(offsets[:]))
@@ -106,12 +119,11 @@ def tile_attend_csoftmaxpool_x_kernel(tc, tab_words, tab_scales, w1, temper, wo,
         w1_scales = [sb(f"w1_scales{t}", [P, P], U8) for t in range(PACK)]
         for h in range(2):
             grouped = sb(f"w1_grouped{h}", [P, PACK, HALF_M, PACK], BF16)
-            split = W1_VECTOR_M if h == 1 else 0
-            if split:
-                o, i = dealt_views(grouped, w1_raw[h], 0, split)
-                nc.vector.tensor_copy(o, i)
-            o, i = dealt_views(grouped, w1_raw[h], split, HALF_M)
-            nc.scalar.copy(o, i)
+            if h == 0:
+                nc.scalar.copy(*dealt_views(grouped, w1_raw[h], 0, PACK))
+            else:
+                nc.vector.tensor_copy(*dealt_views(grouped, w1_raw[h], 0, PACK // 2))
+                nc.scalar.copy(*dealt_views(grouped, w1_raw[h], PACK // 2, PACK))
             cols = slice(h * HALF_M, (h + 1) * HALF_M)
             for t in range(PACK):
                 nc.vector.quantize_mx(
@@ -121,216 +133,183 @@ def tile_attend_csoftmaxpool_x_kernel(tc, tab_words, tab_scales, w1, temper, wo,
                 )
 
         a_banks = [psum.tile([P, 2, J], F32, name=f"a_bank{b}", tag=f"mx{b}") for b in range(2)]
+        a_tiles = [a_banks[t // 2][:, t % 2, :] for t in range(PACK)]
         x = [sb(f"x{t}", [P, G, POOL], F32) for t in range(PACK)]
         for t in range(PACK):
-            nc.tensor.matmul_mx(
-                out=a_banks[t // 2][:, t % 2, :],
-                lhsT=w1_codes[t][:].bitcast(FP8X4),
-                lhsT_scale=w1_scales[t][:],
-                rhs=got_w[:].bitcast(FP4X4),
-                rhs_scale=got_s[:],
-                start=True,
-                stop=True,
-            )
+            product(a_tiles[t], w1_codes[t][:], w1_scales[t][:], got_w[:].bitcast(FP4X4), got_s[:])
         for t in range(PACK):
-            nc.scalar.activation(x[t][:].rearrange("p g q -> p (g q)"), a_banks[t // 2][:, t % 2, :], ACT.Copy, scale=temp[:, t : t + 1])
+            nc.scalar.activation(x[t][:].rearrange("p g q -> p (g q)"), a_tiles[t], ACT.Copy, scale=temper_sb[:, t : t + 1])
 
         top = sb("top", [P, PACK, G], F32)
         below = [sb(f"below{t}", [P, G, POOL], F32) for t in range(PACK)]
-        p_sb = sb("p_sb", [P, PACK, G, POOL], F32)
+        e_sb = sb("e_sb", [P, PACK, G, POOL], F32)
 
         def group_max(t):
             nc.vector.tensor_reduce(top[:, t, :], x[t][:], AX.X, ALU.max)
 
         def shifted_exp(t):
             spread = top[:, t, :].unsqueeze(2).to_broadcast([P, G, POOL])
-            sums = a_banks[t // 2][:, t % 2, :].rearrange("p (g q) -> p g q", q=POOL)
-            nc.vector.scalar_tensor_tensor(below[t][:], sums, temp[:, t : t + 1], spread, ALU.mult, ALU.subtract)
-            nc.scalar.activation(p_sb[:, t, :, :], below[t][:], ACT.Exp)
+            if t == 0:
+                nc.gpsimd.tensor_tensor(below[t][:], x[t][:], spread, ALU.subtract)
+            else:
+                sums = a_tiles[t].rearrange("p (g q) -> p g q", q=POOL)
+                nc.vector.scalar_tensor_tensor(below[t][:], sums, temper_sb[:, t : t + 1], spread, ALU.mult, ALU.subtract)
+            nc.scalar.activation(e_sb[:, t, :, :], below[t][:], ACT.Exp)
 
         group_max(0)
         for t in range(PACK):
             if t + 1 < PACK:
                 group_max(t + 1)
             shifted_exp(t)
-        z_bank = psum.tile([P, 2, P], F32, name="z_bank", tag="turn", bufs=TURN_BANKS)
-        for b in range(2):
-            pooled = p_sb[:, 2 * b : 2 * b + 2, :, :].rearrange("p t g q -> p (t g) q")
-            for q in range(POOL):
-                nc.tensor.matmul(z_bank[:, b, :], pooled[:, :, q], ident[:], start=(q == 0), stop=(q == POOL - 1), is_transpose=True)
-        log_z_turned = sb("log_z_turned", [P, 2, P], F32)
-        nc.scalar.activation(log_z_turned[:], z_bank[:], ACT.Ln)
-        log_z = []
-        for reader in range(2):
-            bank = psum.tile([P, PACK, G], F32, name=f"log_z{reader}", tag="turn", bufs=TURN_BANKS)
-            for b in range(2):
-                nc.tensor.transpose(bank[:, 2 * b : 2 * b + 2, :].rearrange("p t g -> p (t g)"), log_z_turned[:, b, :], ident[:])
-            log_z.append(bank)
 
-        late_grouped = sb("late_grouped", [P, (R + G) * PACK], BF16, tag="w1_grouped1")
-        dy_grouped = late_grouped[:, R * PACK :].rearrange("p (g j) -> p g j", j=PACK)
-        o, i = plain_views(dy_grouped, dy_raw, 0, G // PACK)
-        nc.vector.tensor_copy(o, i)
+        y_bank = turn_bank("y_bank", [P, 2, P])
+        for b in range(2):
+            pooled = e_sb[:, 2 * b : 2 * b + 2, :, :].rearrange("p t g q -> p (t g) q")
+            for q in range(POOL):
+                nc.tensor.matmul(y_bank[:, b, :], pooled[:, :, q], ident[:], start=(q == 0), stop=(q == POOL - 1), is_transpose=True)
+        log_y_turned = sb("log_y_turned", [P, 2, P], F32)
+        nc.scalar.activation(log_y_turned[:], y_bank[:], ACT.Ln)
+
+        def log_y_bank(name):
+            bank = turn_bank(name, [P, PACK, G])
+            for b in range(2):
+                nc.tensor.transpose(bank[:, 2 * b : 2 * b + 2, :].rearrange("p t g -> p (t g)"), log_y_turned[:, b, :], ident[:])
+            return bank
+
+        log_y_vector = log_y_bank("log_y_vector")
+        log_y_scalar = log_y_bank("log_y_scalar")
+
+        late_grouped = sb("late_grouped", [P, (R + G) * PACK], BF16, "w1_grouped1")
+        wo_flat, dy_flat = late_grouped[:, : R * PACK], late_grouped[:, R * PACK :]
+        nc.vector.tensor_copy(*interleaved_views(dy_flat.rearrange("p (g j) -> p g j", j=PACK), dy_raw[:]))
         dy_codes = sb("dy_codes", [P, G], U32)
         dy_scales = sb("dy_scales", [P, G], U8)
-        nc.vector.quantize_mx(out=dy_codes[:].bitcast(FP8X4), scales=dy_scales[:], in_=late_grouped[:, R * PACK :])
-        wo_grouped = late_grouped[:, : R * PACK].rearrange("p (t m j) -> p t m j", t=PACK, j=PACK)
-        o, i = dealt_views(wo_grouped, wo_raw[0], 0, HALF_M)
-        nc.vector.tensor_copy(o, i)
-        for t in range(PACK):
-            nc.gpsimd.tensor_scalar(
-                wo_grouped[:, t, HALF_M:P, :], wo_raw[1][:].rearrange("p j (m t) -> p t m j", t=PACK)[:, t, :, :], 1.0, 0.0, ALU.mult, ALU.add
-            )
-
+        nc.vector.quantize_mx(out=dy_codes[:].bitcast(FP8X4), scales=dy_scales[:], in_=dy_flat)
+        wo_grouped = wo_flat.rearrange("p (t m j) -> p t m j", t=PACK, j=PACK)
+        for h in range(2):
+            nc.vector.tensor_copy(*dealt_views(wo_grouped[:, :, h * HALF_M : (h + 1) * HALF_M, :], wo_raw[h], 0, PACK))
         wo_codes = sb("wo_codes", [P, R], U32)
         wo_scales = sb("wo_scales", [P, R], U8)
-        nc.vector.quantize_mx(out=wo_codes[:].bitcast(FP8X4), scales=wo_scales[:], in_=late_grouped[:, : R * PACK])
-        half_inv = sb("half_inv", [P, PACK], F32)
-        nc.vector.reciprocal(half_inv[:], temp[:])
+        nc.vector.quantize_mx(out=wo_codes[:].bitcast(FP8X4), scales=wo_scales[:], in_=wo_flat)
 
-        half_s = sb("half_s", [P, PACK, G], F32)
-        nc.vector.tensor_tensor(half_s[:], log_z[0][:], top[:], ALU.add)
-        nc.vector.tensor_tensor(half_s[:], half_s[:], half_inv[:].unsqueeze(2).to_broadcast([P, PACK, G]), ALU.mult)
-        inv_z = sb("inv_z", [P, PACK, G], F32)
-        nc.scalar.activation(inv_z[:], log_z[1][:], ACT.Exp, scale=-1.0)
+        inv_temper = sb("inv_temper", [P, PACK], F32)
+        nc.vector.reciprocal(inv_temper[:], temper_sb[:])
+        s_sb = sb("s_sb", [P, PACK, G], F32)
+        nc.vector.tensor_tensor(s_sb[:], log_y_vector[:], top[:], ALU.add)
+        nc.vector.tensor_tensor(s_sb[:], s_sb[:], inv_temper[:].unsqueeze(2).to_broadcast([P, PACK, G]), ALU.mult)
+        fade_wide = sb("fade_wide", [P, HALF_T], F32, "top")
+        nc.sync.dma_start(fade_wide[:], fade[0, 0:HALF_T].partition_broadcast(P))
+        inv_y = sb("inv_y", [P, PACK, G], F32)
         th = sb("th", [P, PACK, G], F32)
-        for h in range(2):
-            groups = slice(h * (G // 2), (h + 1) * (G // 2))
-            nc.scalar.activation(th[:, :, groups], half_s[:, :, groups], ACT.Tanh, scale=one_half[:])
+        group_halves = [slice(h * HALF_G, (h + 1) * HALF_G) for h in range(2)]
+        for groups in group_halves:
+            nc.scalar.activation(inv_y[:, :, groups], log_y_scalar[:, :, groups], ACT.Exp, scale=-1.0)
+            nc.scalar.activation(th[:, :, groups], s_sb[:, :, groups], ACT.Tanh, scale=one_half[:])
 
         c_bank = psum.tile([P, PACK, G], F32, name="c_bank", tag="small")
         for t in range(PACK):
             cols = slice(t * P, (t + 1) * P)
-            nc.tensor.matmul_mx(
-                out=c_bank[:, t, :],
-                lhsT=wo_codes[:, cols].bitcast(FP8X4),
-                lhsT_scale=wo_scales[:, cols],
-                rhs=dy_codes[:].bitcast(FP8X4),
-                rhs_scale=dy_scales[:],
-                start=True,
-                stop=True,
-            )
+            product(c_bank[:, t, :], wo_codes[:, cols], wo_scales[:, cols], dy_codes[:].bitcast(FP8X4), dy_scales[:])
         c_rs = sb("c_rs", [P, PACK, G], F32)
         nc.vector.scalar_tensor_tensor(c_rs[:], c_bank[:], -0.25, rs_sb[:].unsqueeze(2).to_broadcast([P, PACK, G]), ALU.mult, ALU.mult)
 
-        fade_bank = psum.tile([P, P], F32, name="fade_bank", tag="turn", bufs=TURN_BANKS)
+        fade_bank = turn_bank("fade_bank", [P, P])
         nc.tensor.transpose(fade_bank[:], fade_rows[:], ident[:])
-        fade_cols = sb("fade_cols", [P, T // P], F32, "one_half")
-        nc.scalar.copy(fade_cols[:], fade_bank[:, 0 : T // P])
+        fade_cols = sb("fade_cols", [P, CHUNKS], F32, "one_half")
+        nc.scalar.copy(fade_cols[:], fade_bank[:, 0:CHUNKS])
 
         w1r_grouped = sb("w1r_grouped", [P, K, PACK], BF16)
-        o, i = plain_views(w1r_grouped, w1r_raw, 0, K // PACK)
-        nc.vector.tensor_copy(o, i)
+        nc.vector.tensor_copy(*interleaved_views(w1r_grouped[:], w1r_raw[:]))
         w1r_codes = sb("w1r_codes", [P, K], U32)
         w1r_scales = sb("w1r_scales", [P, K], U8)
-
-        def quantize_w1r(a):
-            cols = slice(a * P, (a + 1) * P)
+        k_cols = [slice(a * P, (a + 1) * P) for a in range(K_TILES)]
+        for cols in k_cols:
             nc.vector.quantize_mx(
                 out=w1r_codes[:, cols].bitcast(FP8X4), scales=w1r_scales[:, cols], in_=w1r_grouped[:, cols, :].rearrange("p c j -> p (c j)")
             )
 
-        for a in range(4):
-            quantize_w1r(a)
-
-        c_z = sb("c_z", [P, PACK, G], F32)
-        nc.vector.tensor_tensor(c_z[:], c_rs[:], inv_z[:], ALU.mult)
-        gx = sb("gx", [P, 4, J], F32)
-        GH = G // 2
-        JH = J // 2
-        for h in range(2):
-            groups = slice(h * GH, (h + 1) * GH)
-            v = sb(f"v{h}", [P, PACK, GH], F32)
-            nc.vector.scalar_tensor_tensor(v[:], th[:, :, groups], -1.0, half_s[:, :, groups], ALU.add, ALU.mult)
-            u = sb(f"u{h}", [P, PACK, GH], F32)
-            nc.vector.scalar_tensor_tensor(u[:], th[:, :, groups], 1.0, c_z[:, :, groups], ALU.add, ALU.mult)
-            coef = sb(f"coef{h}", [P, PACK, GH], F32)
-            nc.vector.scalar_tensor_tensor(coef[:], v[:], -2.0, u[:], ALU.add, ALU.mult)
-            gs = sb(f"gs{h}", [P, GH, POOL, PACK], BF16)
+        c_y = sb("c_y", [P, PACK, G], F32)
+        gx = sb("gx", [P, K_TILES, J], F32)
+        for h, (first_tag, rest_tag) in enumerate((("mx0", "mx1"), ("small", "mx0"))):
+            groups = group_halves[h]
+            nc.vector.tensor_tensor(c_y[:, :, groups], c_rs[:, :, groups], inv_y[:, :, groups], ALU.mult)
+            falling = sb(f"falling{h}", [P, PACK, HALF_G], F32)
+            nc.vector.scalar_tensor_tensor(falling[:], th[:, :, groups], -1.0, s_sb[:, :, groups], ALU.add, ALU.mult)
+            rising = sb(f"rising{h}", [P, PACK, HALF_G], F32)
+            nc.vector.scalar_tensor_tensor(rising[:], th[:, :, groups], 1.0, c_y[:, :, groups], ALU.add, ALU.mult)
+            coef = sb(f"coef{h}", [P, PACK, HALF_G], F32)
+            nc.vector.scalar_tensor_tensor(coef[:], falling[:], -2.0, rising[:], ALU.add, ALU.mult)
+            gs = sb(f"gs{h}", [P, HALF_G, POOL, PACK], BF16)
             nc.vector.tensor_tensor(
                 gs[:].rearrange("p g q t -> p g t q"),
-                p_sb[:, :, groups, :].rearrange("p t g q -> p g t q"),
-                coef[:].rearrange("p t g -> p g t").unsqueeze(3).to_broadcast([P, GH, PACK, POOL]),
+                e_sb[:, :, groups, :].rearrange("p t g q -> p g t q"),
+                coef[:].rearrange("p t g -> p g t").unsqueeze(3).to_broadcast([P, HALF_G, PACK, POOL]),
                 ALU.mult,
             )
-            gs_codes = sb(f"gs_codes{h}", [P, JH], U32)
-            gs_scales = sb(f"gs_scales{h}", [P, JH], U8)
+            gs_codes = sb(f"gs_codes{h}", [P, HALF_J], U32)
+            gs_scales = sb(f"gs_scales{h}", [P, HALF_J], U8)
             nc.vector.quantize_mx(out=gs_codes[:].bitcast(FP8X4), scales=gs_scales[:], in_=gs[:].rearrange("p g q t -> p (g q t)"))
-            if h == 0:
-                first = psum.tile([P, 1, JH], F32, name="gx_first0", tag="mx0")
-                rest = psum.tile([P, 3, JH], F32, name="gx_rest0", tag="mx1")
-            else:
-                first = psum.tile([P, 1, JH], F32, name="gx_first1", tag="small")
-                rest = psum.tile([P, 3, JH], F32, name="gx_rest1", tag="mx0")
-            for a in range(4):
-                cols = slice(a * P, (a + 1) * P)
-                nc.tensor.matmul_mx(
-                    out=first[:, 0, :] if a == 0 else rest[:, a - 1, :],
-                    lhsT=w1r_codes[:, cols].bitcast(FP8X4),
-                    lhsT_scale=w1r_scales[:, cols],
-                    rhs=gs_codes[:].bitcast(FP8X4),
-                    rhs_scale=gs_scales[:],
-                    start=True,
-                    stop=True,
-                )
-            slots = slice(h * JH, (h + 1) * JH)
+            first = psum.tile([P, 1, HALF_J], F32, name=f"gx_first{h}", tag=first_tag)
+            rest = psum.tile([P, K_TILES - 1, HALF_J], F32, name=f"gx_rest{h}", tag=rest_tag)
+            for a, cols in enumerate(k_cols):
+                place = first[:, 0, :] if a == 0 else rest[:, a - 1, :]
+                product(place, w1r_codes[:, cols], w1r_scales[:, cols], gs_codes[:].bitcast(FP8X4), gs_scales[:])
+            slots = slice(h * HALF_J, (h + 1) * HALF_J)
             nc.scalar.copy(gx[:, 0:1, slots], first[:])
-            nc.scalar.copy(gx[:, 1:4, slots], rest[:])
+            nc.scalar.copy(gx[:, 1:K_TILES, slots], rest[:])
 
-        for a, tag in ((2, "gs0"), (3, "gs_codes1")):
-            windows.append(sb(f"window{a}", [P, T], F32, tag))
-            nc.gpsimd.memset(windows[a][:], 0.0)
-
-        faded_t = [sb(f"faded_t{c}", [P, K], F32) for c in range(T // P)]
+        faded_turned = [sb(f"faded_turned{c}", [P, K], F32) for c in range(CHUNKS)]
+        chunks_in_half = CHUNKS // 2
 
         def fade_chunk(c):
-            bank = psum.tile([P, K], F32, name=f"turn{c}", tag="turn", bufs=TURN_BANKS)
-            first_tile = 1 if c < 4 else 0
-            for a in range(first_tile, 4):
-                nc.tensor.transpose(bank[:, a * P : (a + 1) * P], old_sb[c // 4][:, a, (c % 4) * P : (c % 4 + 1) * P], ident[:])
+            h, place = divmod(c, chunks_in_half)
+            first_tile = 1 if h == 0 else 0
+            bank = turn_bank(f"turn{c}", [P, K])
+            for a in range(first_tile, K_TILES):
+                nc.tensor.transpose(bank[:, k_cols[a]], old_sb[h][:, a, place * P : (place + 1) * P], ident[:])
             rows = slice(first_tile * P, K)
-            nc.scalar.activation(faded_t[c][:, rows], bank[:, rows], ACT.Copy, scale=fade_cols[:, c : c + 1])
+            nc.scalar.activation(faded_turned[c][:, rows], bank[:, rows], ACT.Copy, scale=fade_cols[:, c : c + 1])
 
-        def turn_back(a, h, tag, bufs=1):
-            bank = psum.tile([P, T // 2], F32, name=f"back{a}_{h}", tag=tag, bufs=bufs)
-            for c in range(4):
-                nc.tensor.transpose(bank[:, c * P : (c + 1) * P], faded_t[4 * h + c][:, a * P : (a + 1) * P], ident[:])
+        def turn_back(a, h, tag=""):
+            name = f"back{a}_{h}"
+            bank = psum.tile([P, HALF_T], F32, name=name, tag=tag) if tag else turn_bank(name, [P, HALF_T])
+            for place in range(chunks_in_half):
+                nc.tensor.transpose(bank[:, place * P : (place + 1) * P], faded_turned[chunks_in_half * h + place][:, k_cols[a]], ident[:])
             return bank
 
-        def finish(a, c0, c1, engine, faded, tag=""):
-            result = sb(f"result{a}_{c0}", [P, c1 - c0], F32, tag)
-            engine.tensor_tensor(result[:], faded, windows[a][:, c0:c1], ALU.add)
-            nc.sync.dma_start(out[a * P : (a + 1) * P, c0:c1], result[:])
+        def finish(a, t0, t1, engine, faded, reuse=""):
+            result = sb(f"result{a}_{t0}", [P, t1 - t0], F32, reuse)
+            engine.tensor_tensor(result[:], faded, windows[a][:, t0:t1], ALU.add)
+            nc.sync.dma_start(out[k_cols[a], t0:t1], result[:])
 
-        def finish_on_gpsimd(a, c0, c1, source):
-            faded = sb(f"faded{a}_{c0}", [P, c1 - c0], F32)
+        def finish_on_gpsimd(a, t0, t1, source):
+            faded = sb(f"faded{a}_{t0}", [P, t1 - t0], F32)
             nc.scalar.copy(faded[:], source)
-            finish(a, c0, c1, nc.gpsimd, faded[:])
+            finish(a, t0, t1, nc.gpsimd, faded[:])
 
-        def scatter(a, h0, h1):
-            nc.vector.tensor_copy(windows[a][:].indirect(offsets[:, 8 * h0 : 8 * h1]), gx[:, a, h0 * JH : h1 * JH])
+        def scatter(a, j0, j1):
+            nc.vector.tensor_copy(windows[a][:].indirect(offsets[:, j0 // LIST_ROWS : j1 // LIST_ROWS]), gx[:, a, j0:j1])
 
-        H, Q = T // 2, T // 4
-        scatter(0, 0, 1)
-        scatter(0, 1, 2)
-        scatter(1, 0, 2)
-        scatter(2, 0, 2)
-        for c in range(4):
+        scatter(0, 0, HALF_J)
+        scatter(0, HALF_J, J)
+        scatter(1, 0, J)
+        scatter(2, 0, J)
+        for c in range(chunks_in_half):
             fade_chunk(c)
-        faded = sb("faded0_0", [P, H], F32, "gs1")
-        nc.gpsimd.tensor_tensor(faded[:], old_sb[0][:, 0, :], fade_wide[:], ALU.mult)
-        finish(0, 0, H, nc.gpsimd, faded[:])
-        for c in range(4, 8):
+        faded_direct = sb("faded_direct", [P, HALF_T], F32, "gs1")
+        nc.gpsimd.tensor_tensor(faded_direct[:], old_sb[0][:, 0, :], fade_wide[:], ALU.mult)
+        finish(0, 0, HALF_T, nc.gpsimd, faded_direct[:])
+        for c in range(chunks_in_half, CHUNKS):
             fade_chunk(c)
-        finish_on_gpsimd(1, 0, H, turn_back(1, 0, "small")[:])
-        finish_on_gpsimd(0, H, T, turn_back(0, 1, "turn", TURN_BANKS)[:])
-        finish_on_gpsimd(1, H, T, turn_back(1, 1, "turn", TURN_BANKS)[:])
-        bank = turn_back(2, 0, "mx1")
-        finish_on_gpsimd(2, 0, Q, bank[:, 0:Q])
-        finish(2, Q, H, nc.vector, bank[:, Q:H], "faded1_0")
-        finish(2, H, T, nc.vector, turn_back(2, 1, "small")[:])
-        scatter(3, 0, 2)
-        finish(3, 0, H, nc.vector, turn_back(3, 0, "mx0")[:], "faded1_512")
-        bank = turn_back(3, 1, "turn", TURN_BANKS)
-        finish(3, H, H + Q, nc.vector, bank[:, 0:Q])
-        finish(3, H + Q, T, nc.vector, bank[:, Q:H])
+        finish_on_gpsimd(1, 0, HALF_T, turn_back(1, 0, "small")[:])
+        finish_on_gpsimd(0, HALF_T, T, turn_back(0, 1)[:])
+        finish_on_gpsimd(1, HALF_T, T, turn_back(1, 1)[:])
+        low_bank = turn_back(2, 0, "mx1")
+        finish_on_gpsimd(2, 0, QUARTER_T, low_bank[:, 0:QUARTER_T])
+        finish(2, QUARTER_T, HALF_T, nc.vector, low_bank[:, QUARTER_T:HALF_T], "faded1_0")
+        finish(2, HALF_T, T, nc.vector, turn_back(2, 1, "small")[:])
+        scatter(3, 0, J)
+        finish(3, 0, HALF_T, nc.vector, turn_back(3, 0, "mx0")[:], f"faded1_{HALF_T}")
+        high_bank = turn_back(3, 1)
+        finish(3, HALF_T, HALF_T + QUARTER_T, nc.vector, high_bank[:, 0:QUARTER_T])
+        finish(3, HALF_T + QUARTER_T, T, nc.vector, high_bank[:, QUARTER_T:HALF_T])

from contextlib import ExitStack

import concourse.mybir as mybir
from concourse.masks import make_identity

K, R, F, T, J, G = 512, 512, 512, 1024, 256, 64
FLOPS = 2 * (K * R * J + F * R * G + R * K * J)

F32 = mybir.dt.float32
BF16 = mybir.dt.bfloat16
I32 = mybir.dt.int32
U32 = mybir.dt.uint32
U16 = mybir.dt.uint16
U8 = mybir.dt.uint8
FP8X4 = mybir.dt.float8_e4m3fn_x4
FP4X4 = mybir.dt.float4_e2m1fn_x4
ACT = mybir.ActivationFunctionType
ALU = mybir.AluOpType
AX = mybir.AxisListType

P = 128
PACK = 4
POOL = J // G
K_TILES = K // P
CHUNKS = T // P
QUADRANT = 32
LIST_ROWS = 16
HALF_M = P // 2
HALF_R = R // 2
HALF_G = G // 2
HALF_J = J // 2
HALF_T = T // 2
QUARTER_T = T // 4
TURN_BANKS = 5


def dealt_views(grouped, raw, t0, t1):
    out = grouped[:, t0:t1, :, :].rearrange("p t (n e) j -> p n j e t", e=2)
    in_ = raw[:].rearrange("p j (n e t) -> p n j e t", e=2, t=PACK)[:, :, :, :, t0:t1]
    return out, in_


def interleaved_views(grouped, raw):
    out = grouped.rearrange("p (n i) j -> p n j i", i=PACK)
    in_ = raw.rearrange("p j (n i) -> p n j i", i=PACK)
    return out, in_


def tile_attend_csoftmaxpool_x_kernel(tc, tab_words, tab_scales, w1, temper, wo, dy, rs, w1r, old, fade, offs, out):
    nc = tc.nc
    with ExitStack() as ctx:
        keep = ctx.enter_context(tc.tile_pool(name="keep", bufs=1))
        psum = ctx.enter_context(tc.psum_pool(name="psum", bufs=1))

        def sb(name, shape, dtype, reuse=""):
            return keep.tile(shape, dtype, name=name, align_bytes=64, tag=reuse or name)

        def turn_bank(name, shape):
            return psum.tile(shape, F32, name=name, tag="turn", bufs=TURN_BANKS)

        def product(out_ap, codes, scales, moving_codes, moving_scales):
            nc.tensor.matmul_mx(
                out=out_ap, lhsT=codes.bitcast(FP8X4), lhsT_scale=scales, rhs=moving_codes, rhs_scale=moving_scales, start=True, stop=True
            )

        offsets = keep.tile([P, J // LIST_ROWS], U16, name="offsets")
        nc.sync.dma_start(offsets[:], offs)
        tab_s = sb("tab_s", [P, T], U8)
        nc.vector.memset(tab_s[:].bitcast(I32), 0)
        scale_rows = sb("scale_rows", [P, T // 4], I32)
        live_rows = [slice(QUADRANT * q, QUADRANT * q + 4) for q in range(P // QUADRANT)]
        for q, rows in enumerate(live_rows):
            nc.scalar.dma_start(scale_rows[rows, :], tab_scales[0, 4 * q : 4 * q + 4, :].bitcast(I32))
        tab_w = sb("tab_w", [P, T], U16)
        nc.sync.dma_start(tab_w[:].bitcast(I32), tab_words[0].bitcast(I32))

        def load_rows(name, source):
            raw = sb(name, [P, PACK, source.shape[1]], F32)
            nc.sync.dma_start(raw[:], source.rearrange("(p j) c -> p j c", j=PACK))
            return raw

        def load_by_feature(name, source):
            tile = sb(name, [P, PACK], F32)
            nc.sync.dma_start(tile[:], source.rearrange("(p t) o -> p (t o)", t=PACK))
            return tile

        w1_raw = [load_rows(f"w1_raw{h}", w1[:, h * HALF_R : (h + 1) * HALF_R]) for h in range(2)]
        temper_sb = load_by_feature("temper_sb", temper)
        dy_raw = load_rows("dy_raw", dy)
        wo_raw = [load_rows(f"wo_raw{h}", wo[:, h * HALF_R : (h + 1) * HALF_R]) for h in range(2)]
        w1r_raw = load_rows("w1r_raw", w1r)
        rs_sb = load_by_feature("rs_sb", rs)
        fade_rows = sb("fade_rows", [P, P], F32)
        nc.gpsimd.memset(fade_rows[:], 0.0)
        nc.sync.dma_start(fade_rows[0:CHUNKS, :], fade.rearrange("o (c p) -> (o c) p", p=P))
        old_sb = []
        for h in range(2):
            old_half = sb(f"old{h}", [P, K_TILES, HALF_T], F32)
            nc.sync.dma_start(old_half[:], old[:, h * HALF_T : (h + 1) * HALF_T].rearrange("(a p) c -> p a c", p=P))
            old_sb.append(old_half)

        ident = sb("ident", [P, P], F32)
        make_identity(nc, ident[:])
        one_half = sb("one_half", [P, 1], F32)
        nc.gpsimd.memset(one_half[:], 0.5)

        windows = [sb(f"window{a}", [P, T], F32) for a in range(K_TILES)]
        for window in windows:
            nc.vector.memset(window[:].bitcast(I32), 0)
        for rows in live_rows:
            nc.vector.tensor_copy(tab_s[rows, :].bitcast(I32), scale_rows[rows, :])

        got_w = sb("got_w", [P, J], U16)
        nc.vector.tensor_copy(got_w[:], tab_w[:].indirect(offsets[:]))
        got_s = sb("got_s", [P, J], U8)
        nc.vector.tensor_copy(got_s[:], tab_s[:].indirect(offsets[:]))

        w1_codes = [sb(f"w1_codes{t}", [P, P], U32) for t in range(PACK)]
        w1_scales = [sb(f"w1_scales{t}", [P, P], U8) for t in range(PACK)]
        for h in range(2):
            grouped = sb(f"w1_grouped{h}", [P, PACK, HALF_M, PACK], BF16)
            if h == 0:
                nc.scalar.copy(*dealt_views(grouped, w1_raw[h], 0, PACK))
            else:
                nc.vector.tensor_copy(*dealt_views(grouped, w1_raw[h], 0, PACK // 2))
                nc.scalar.copy(*dealt_views(grouped, w1_raw[h], PACK // 2, PACK))
            cols = slice(h * HALF_M, (h + 1) * HALF_M)
            for t in range(PACK):
                nc.vector.quantize_mx(
                    out=w1_codes[t][:, cols].bitcast(FP8X4),
                    scales=w1_scales[t][:, cols],
                    in_=grouped[:, t, :, :].rearrange("p m j -> p (m j)"),
                )

        a_banks = [psum.tile([P, 2, J], F32, name=f"a_bank{b}", tag=f"mx{b}") for b in range(2)]
        a_tiles = [a_banks[t // 2][:, t % 2, :] for t in range(PACK)]
        x = [sb(f"x{t}", [P, G, POOL], F32) for t in range(PACK)]
        for t in range(PACK):
            product(a_tiles[t], w1_codes[t][:], w1_scales[t][:], got_w[:].bitcast(FP4X4), got_s[:])
        for t in range(PACK):
            nc.scalar.activation(x[t][:].rearrange("p g q -> p (g q)"), a_tiles[t], ACT.Copy, scale=temper_sb[:, t : t + 1])

        top = sb("top", [P, PACK, G], F32)
        below = [sb(f"below{t}", [P, G, POOL], F32) for t in range(PACK)]
        e_sb = sb("e_sb", [P, PACK, G, POOL], F32)

        def group_max(t):
            nc.vector.tensor_reduce(top[:, t, :], x[t][:], AX.X, ALU.max)

        def shifted_exp(t):
            spread = top[:, t, :].unsqueeze(2).to_broadcast([P, G, POOL])
            if t == 0:
                nc.gpsimd.tensor_tensor(below[t][:], x[t][:], spread, ALU.subtract)
            else:
                sums = a_tiles[t].rearrange("p (g q) -> p g q", q=POOL)
                nc.vector.scalar_tensor_tensor(below[t][:], sums, temper_sb[:, t : t + 1], spread, ALU.mult, ALU.subtract)
            nc.scalar.activation(e_sb[:, t, :, :], below[t][:], ACT.Exp)

        group_max(0)
        for t in range(PACK):
            if t + 1 < PACK:
                group_max(t + 1)
            shifted_exp(t)

        y_bank = turn_bank("y_bank", [P, 2, P])
        for b in range(2):
            pooled = e_sb[:, 2 * b : 2 * b + 2, :, :].rearrange("p t g q -> p (t g) q")
            for q in range(POOL):
                nc.tensor.matmul(y_bank[:, b, :], pooled[:, :, q], ident[:], start=(q == 0), stop=(q == POOL - 1), is_transpose=True)
        log_y_turned = sb("log_y_turned", [P, 2, P], F32)
        nc.scalar.activation(log_y_turned[:], y_bank[:], ACT.Ln)

        def log_y_bank(name):
            bank = turn_bank(name, [P, PACK, G])
            for b in range(2):
                nc.tensor.transpose(bank[:, 2 * b : 2 * b + 2, :].rearrange("p t g -> p (t g)"), log_y_turned[:, b, :], ident[:])
            return bank

        log_y_vector = log_y_bank("log_y_vector")
        log_y_scalar = log_y_bank("log_y_scalar")

        late_grouped = sb("late_grouped", [P, (R + G) * PACK], BF16, "w1_grouped1")
        wo_flat, dy_flat = late_grouped[:, : R * PACK], late_grouped[:, R * PACK :]
        nc.vector.tensor_copy(*interleaved_views(dy_flat.rearrange("p (g j) -> p g j", j=PACK), dy_raw[:]))
        dy_codes = sb("dy_codes", [P, G], U32)
        dy_scales = sb("dy_scales", [P, G], U8)
        nc.vector.quantize_mx(out=dy_codes[:].bitcast(FP8X4), scales=dy_scales[:], in_=dy_flat)
        wo_grouped = wo_flat.rearrange("p (t m j) -> p t m j", t=PACK, j=PACK)
        for h in range(2):
            nc.vector.tensor_copy(*dealt_views(wo_grouped[:, :, h * HALF_M : (h + 1) * HALF_M, :], wo_raw[h], 0, PACK))
        wo_codes = sb("wo_codes", [P, R], U32)
        wo_scales = sb("wo_scales", [P, R], U8)
        nc.vector.quantize_mx(out=wo_codes[:].bitcast(FP8X4), scales=wo_scales[:], in_=wo_flat)

        inv_temper = sb("inv_temper", [P, PACK], F32)
        nc.vector.reciprocal(inv_temper[:], temper_sb[:])
        s_sb = sb("s_sb", [P, PACK, G], F32)
        nc.vector.tensor_tensor(s_sb[:], log_y_vector[:], top[:], ALU.add)
        nc.vector.tensor_tensor(s_sb[:], s_sb[:], inv_temper[:].unsqueeze(2).to_broadcast([P, PACK, G]), ALU.mult)
        fade_wide = sb("fade_wide", [P, HALF_T], F32, "top")
        nc.sync.dma_start(fade_wide[:], fade[0, 0:HALF_T].partition_broadcast(P))
        inv_y = sb("inv_y", [P, PACK, G], F32)
        th = sb("th", [P, PACK, G], F32)
        group_halves = [slice(h * HALF_G, (h + 1) * HALF_G) for h in range(2)]
        for groups in group_halves:
            nc.scalar.activation(inv_y[:, :, groups], log_y_scalar[:, :, groups], ACT.Exp, scale=-1.0)
            nc.scalar.activation(th[:, :, groups], s_sb[:, :, groups], ACT.Tanh, scale=one_half[:])

        c_bank = psum.tile([P, PACK, G], F32, name="c_bank", tag="small")
        for t in range(PACK):
            cols = slice(t * P, (t + 1) * P)
            product(c_bank[:, t, :], wo_codes[:, cols], wo_scales[:, cols], dy_codes[:].bitcast(FP8X4), dy_scales[:])
        c_rs = sb("c_rs", [P, PACK, G], F32)
        nc.vector.scalar_tensor_tensor(c_rs[:], c_bank[:], -0.25, rs_sb[:].unsqueeze(2).to_broadcast([P, PACK, G]), ALU.mult, ALU.mult)

        fade_bank = turn_bank("fade_bank", [P, P])
        nc.tensor.transpose(fade_bank[:], fade_rows[:], ident[:])
        fade_cols = sb("fade_cols", [P, CHUNKS], F32, "one_half")
        nc.scalar.copy(fade_cols[:], fade_bank[:, 0:CHUNKS])

        w1r_grouped = sb("w1r_grouped", [P, K, PACK], BF16)
        nc.vector.tensor_copy(*interleaved_views(w1r_grouped[:], w1r_raw[:]))
        w1r_codes = sb("w1r_codes", [P, K], U32)
        w1r_scales = sb("w1r_scales", [P, K], U8)
        k_cols = [slice(a * P, (a + 1) * P) for a in range(K_TILES)]
        for cols in k_cols:
            nc.vector.quantize_mx(
                out=w1r_codes[:, cols].bitcast(FP8X4), scales=w1r_scales[:, cols], in_=w1r_grouped[:, cols, :].rearrange("p c j -> p (c j)")
            )

        c_y = sb("c_y", [P, PACK, G], F32)
        gx = sb("gx", [P, K_TILES, J], F32)
        for h, (first_tag, rest_tag) in enumerate((("mx0", "mx1"), ("small", "mx0"))):
            groups = group_halves[h]
            nc.vector.tensor_tensor(c_y[:, :, groups], c_rs[:, :, groups], inv_y[:, :, groups], ALU.mult)
            falling = sb(f"falling{h}", [P, PACK, HALF_G], F32)
            nc.vector.scalar_tensor_tensor(falling[:], th[:, :, groups], -1.0, s_sb[:, :, groups], ALU.add, ALU.mult)
            rising = sb(f"rising{h}", [P, PACK, HALF_G], F32)
            nc.vector.scalar_tensor_tensor(rising[:], th[:, :, groups], 1.0, c_y[:, :, groups], ALU.add, ALU.mult)
            coef = sb(f"coef{h}", [P, PACK, HALF_G], F32)
            nc.vector.scalar_tensor_tensor(coef[:], falling[:], -2.0, rising[:], ALU.add, ALU.mult)
            gs = sb(f"gs{h}", [P, HALF_G, POOL, PACK], BF16)
            nc.vector.tensor_tensor(
                gs[:].rearrange("p g q t -> p g t q"),
                e_sb[:, :, groups, :].rearrange("p t g q -> p g t q"),
                coef[:].rearrange("p t g -> p g t").unsqueeze(3).to_broadcast([P, HALF_G, PACK, POOL]),
                ALU.mult,
            )
            gs_codes = sb(f"gs_codes{h}", [P, HALF_J], U32)
            gs_scales = sb(f"gs_scales{h}", [P, HALF_J], U8)
            nc.vector.quantize_mx(out=gs_codes[:].bitcast(FP8X4), scales=gs_scales[:], in_=gs[:].rearrange("p g q t -> p (g q t)"))
            first = psum.tile([P, 1, HALF_J], F32, name=f"gx_first{h}", tag=first_tag)
            rest = psum.tile([P, K_TILES - 1, HALF_J], F32, name=f"gx_rest{h}", tag=rest_tag)
            for a, cols in enumerate(k_cols):
                place = first[:, 0, :] if a == 0 else rest[:, a - 1, :]
                product(place, w1r_codes[:, cols], w1r_scales[:, cols], gs_codes[:].bitcast(FP8X4), gs_scales[:])
            slots = slice(h * HALF_J, (h + 1) * HALF_J)
            nc.scalar.copy(gx[:, 0:1, slots], first[:])
            nc.scalar.copy(gx[:, 1:K_TILES, slots], rest[:])

        faded_turned = [sb(f"faded_turned{c}", [P, K], F32) for c in range(CHUNKS)]
        chunks_in_half = CHUNKS // 2

        def fade_chunk(c):
            h, place = divmod(c, chunks_in_half)
            first_tile = 1 if h == 0 else 0
            bank = turn_bank(f"turn{c}", [P, K])
            for a in range(first_tile, K_TILES):
                nc.tensor.transpose(bank[:, k_cols[a]], old_sb[h][:, a, place * P : (place + 1) * P], ident[:])
            rows = slice(first_tile * P, K)
            nc.scalar.activation(faded_turned[c][:, rows], bank[:, rows], ACT.Copy, scale=fade_cols[:, c : c + 1])

        def turn_back(a, h, tag=""):
            name = f"back{a}_{h}"
            bank = psum.tile([P, HALF_T], F32, name=name, tag=tag) if tag else turn_bank(name, [P, HALF_T])
            for place in range(chunks_in_half):
                nc.tensor.transpose(bank[:, place * P : (place + 1) * P], faded_turned[chunks_in_half * h + place][:, k_cols[a]], ident[:])
            return bank

        def finish(a, t0, t1, engine, faded, reuse=""):
            result = sb(f"result{a}_{t0}", [P, t1 - t0], F32, reuse)
            engine.tensor_tensor(result[:], faded, windows[a][:, t0:t1], ALU.add)
            nc.sync.dma_start(out[k_cols[a], t0:t1], result[:])

        def finish_on_gpsimd(a, t0, t1, source):
            faded = sb(f"faded{a}_{t0}", [P, t1 - t0], F32)
            nc.scalar.copy(faded[:], source)
            finish(a, t0, t1, nc.gpsimd, faded[:])

        def scatter(a, j0, j1):
            nc.vector.tensor_copy(windows[a][:].indirect(offsets[:, j0 // LIST_ROWS : j1 // LIST_ROWS]), gx[:, a, j0:j1])

        scatter(0, 0, HALF_J)
        scatter(0, HALF_J, J)
        scatter(1, 0, J)
        scatter(2, 0, J)
        for c in range(chunks_in_half):
            fade_chunk(c)
        faded_direct = sb("faded_direct", [P, HALF_T], F32, "gs1")
        nc.gpsimd.tensor_tensor(faded_direct[:], old_sb[0][:, 0, :], fade_wide[:], ALU.mult)
        finish(0, 0, HALF_T, nc.gpsimd, faded_direct[:])
        for c in range(chunks_in_half, CHUNKS):
            fade_chunk(c)
        finish_on_gpsimd(1, 0, HALF_T, turn_back(1, 0, "small")[:])
        finish_on_gpsimd(0, HALF_T, T, turn_back(0, 1)[:])
        finish_on_gpsimd(1, HALF_T, T, turn_back(1, 1)[:])
        low_bank = turn_back(2, 0, "mx1")
        finish_on_gpsimd(2, 0, QUARTER_T, low_bank[:, 0:QUARTER_T])
        finish(2, QUARTER_T, HALF_T, nc.vector, low_bank[:, QUARTER_T:HALF_T], "faded1_0")
        finish(2, HALF_T, T, nc.vector, turn_back(2, 1, "small")[:])
        scatter(3, 0, J)
        finish(3, 0, HALF_T, nc.vector, turn_back(3, 0, "mx0")[:], f"faded1_{HALF_T}")
        high_bank = turn_back(3, 1)
        finish(3, HALF_T, HALF_T + QUARTER_T, nc.vector, high_bank[:, 0:QUARTER_T])
        finish(3, HALF_T + QUARTER_T, T, nc.vector, high_bank[:, QUARTER_T:HALF_T])
